import numpy as np
import ml_dtypes


def mxq(x, axis, fmt="e4m3"):
    dtype, down = {"e4m3": (ml_dtypes.float8_e4m3fn, 7), "e5m2": (ml_dtypes.float8_e5m2, 14)}[fmt]
    v = np.moveaxis(np.asarray(x, np.float32).astype(ml_dtypes.bfloat16).astype(np.float64), axis, -1)
    blocks = v.reshape(v.shape[:-1] + (-1, 32))
    amax = np.abs(blocks).max(-1, keepdims=True)
    byte = np.maximum(np.where(amax > 0, np.frexp(amax)[1] - 1 + 127, 0) - down, 1)
    scale = np.exp2(byte - 127.0)
    codes = (blocks / scale).astype(np.float32).astype(dtype).astype(np.float64)
    return np.moveaxis((codes * scale).reshape(v.shape), -1, axis)


WIDE = False


def mx_kscale(k):
    if not WIDE:
        return np.ones(k)
    levels = np.array([10, -10, 5, -5, 0])
    if k % 512:
        return np.exp2(np.random.permutation(np.resize(levels, k // 32))).repeat(32)
    a = np.empty((k // 512, 16))
    for p in range(k // 512):
        a[p, :8] = np.random.permutation(np.resize(levels, 8))
        for g in range(8):
            far = levels[np.abs(levels - a[p, g]) >= 10]
            a[p, g + 8] = far[np.random.randint(len(far))]
    return np.exp2(a.ravel()).repeat(32)


def f64(x):
    return np.asarray(x).astype(np.float64)


def striped(idx):
    return np.tile(idx.reshape(-1, 16).T, (8, 1)).astype(np.uint16)


def unstriped(offs):
    return offs[:16].T.reshape(-1).astype(np.int64)


E2M1 = np.array([0.0, 0.5, 1.0, 1.5, 2.0, 3.0, 4.0, 6.0, -0.0, -0.5, -1.0, -1.5, -2.0, -3.0, -4.0, -6.0])


def pack_weight(w, fmt):
    k, n = w.shape
    w = f64(np.asarray(w, np.float32).astype(ml_dtypes.bfloat16)).reshape(k // 32, 32, n)
    amax = np.abs(w).max(1)
    if fmt == "e4m3":
        byte = np.frexp(amax)[1] - 1 + 127 - 7
    else:
        mant, ex = np.frexp(amax / 6.0)
        byte = np.where(mant > 0.5, ex, ex - 1) + 127
    byte = np.clip(np.where(amax > 0, byte, 1), 1, 254)
    scaled = (w * np.exp2(127.0 - byte)[:, None, :]).reshape(k, n).astype(np.float32)
    by_word = np.ascontiguousarray(scaled.reshape(k // 512, 128, 4, n).transpose(0, 1, 3, 2))
    if fmt == "e4m3":
        words = by_word.astype(ml_dtypes.float8_e4m3fn).view(np.uint8)
    else:
        c = by_word.astype(ml_dtypes.float4_e2m1fn).view(np.uint8) & 0xF
        words = (c[..., 0::2] | (c[..., 1::2] << 4)).reshape(k // 512, 128, 2 * n)
    return np.ascontiguousarray(words), np.ascontiguousarray(byte.astype(np.uint8).reshape(k // 512, 16, n))


def unpack_weight(words, scales, fmt):
    g, _, n = scales.shape
    words = np.ascontiguousarray(words).reshape(g, 128, n, -1)
    if fmt == "e4m3":
        vals = words.view(ml_dtypes.float8_e4m3fn).astype(np.float64)
    else:
        nib = np.empty((g, 128, n, 4), np.uint8)
        nib[..., 0::2] = words & 0xF
        nib[..., 1::2] = words >> 4
        vals = E2M1[nib]
    vals = vals * np.repeat(np.exp2(scales.astype(np.float64) - 127.0), 8, axis=1)[..., None]
    return vals.transpose(0, 1, 3, 2).reshape(g * 512, n)


def relu(v):
    return np.maximum(v, 0.0)


K, T, E, C, N = 1024, 1280, 8, 128, 256


def by_expert(wq, xq):
    return np.concatenate([wq[e].T @ xq[:, e * C:(e + 1) * C] for e in range(E)], axis=1)


def setup_inputs():
    n = np.random.standard_normal
    s = mx_kscale(K)[:, None]
    w = [pack_weight(m, "e2m1") for m in n((E, K, N)) / np.sqrt(K) / s[None]]
    return {
        "xT": (n((K, T)) * s).astype(np.float32),
        "w_words": np.stack([m[0] for m in w]),
        "w_scales": np.stack([m[1] for m in w]),
        "b": (0.3 * n((N, E))).astype(np.float32),
        "gate": np.tile(np.random.uniform(0.2, 1.0, E * C), (N, 1)).astype(np.float32),
        "offs": striped(np.random.permutation(T)[:E * C]),
        "dst": striped(np.random.permutation(T)[:E * C]),
    }


def reference(xT, w_words, w_scales, b, gate, offs, dst):
    idx = unstriped(offs)
    w = np.stack([unpack_weight(w_words[e], w_scales[e], "e2m1") for e in range(E)])
    xq = mxq(f64(xT)[:, idx], 0, "e4m3")
    y = by_expert(w, xq)
    y = relu(y + np.repeat(f64(b), C, axis=1))
    out = np.zeros((N, T))
    out[:, unstriped(dst)] = f64(gate) * y
    return out

@@ -1,0 +1,154 @@
+from contextlib import ExitStack
+
+import concourse.mybir as mybir
+
+K, T, E, C, N = 1024, 1280, 8, 128, 256
+SLOTS = E * C
+FLOPS = 2 * K * SLOTS * N
+P = 128
+PACK = 4
+PASSES = K // (P * PACK)
+HALVES = N // P
+
+F32 = mybir.dt.float32
+BF16 = mybir.dt.bfloat16
+I32 = mybir.dt.int32
+U32 = mybir.dt.uint32
+U16 = mybir.dt.uint16
+U8 = mybir.dt.uint8
+FP8X4 = mybir.dt.float8_e4m3fn_x4
+FP4X4 = mybir.dt.float4_e2m1fn_x4
+COPY = mybir.ActivationFunctionType.Copy
+RELU = mybir.ActivationFunctionType.Relu
+MULT = mybir.AluOpType.mult
+
+CHUNKS = (
+    ((0, 256, 160), (256, 512, 336), (768, 256, 192), (1024, 256, 192)),
+    ((0, 512, 0), (512, 512, 64), (1024, 256, 128)),
+)
+PIECE = 512
+
+
+def interleave(copy, grouped, raw, a, b):
+    copy(
+        grouped[:, a:b, :].rearrange("p (c i) t -> p c t i", i=4),
+        raw[:, :, a:b].rearrange("p t (c i) -> p c t i", i=4),
+    )
+
+
+def tile_moe_two_lin_relu_kernel(tc, xT, w_words, w_scales, b, gate, offs, dst, out):
+    nc = tc.nc
+    with ExitStack() as ctx:
+        keep = ctx.enter_context(tc.tile_pool(name="keep", bufs=1))
+        psum = ctx.enter_context(tc.psum_pool(name="psum", bufs=1))
+
+        offs_t = keep.tile([P, SLOTS // 16], U16, name="offs_t")
+        dst_t = keep.tile([P, SLOTS // 16], U16, name="dst_t")
+        ww = keep.tile([P, E * PASSES, 2 * N], U8, name="ww", align_bytes=64)
+        ws = keep.tile([P, E * PASSES, N], U8, name="ws", align_bytes=64)
+        gate_t = [keep.tile([P, SLOTS], F32, name=f"gate{h}") for h in range(HALVES)]
+        bias = keep.tile([P, HALVES, E], F32, name="bias")
+        out_t = [keep.tile([P, T], F32, name=f"out{h}") for h in range(HALVES)]
+        codes = [keep.tile([P, T], U32, name=f"codes{a}", align_bytes=64) for a in range(PASSES)]
+        planes = [keep.tile([P, T], U8, name=f"planes{a}", align_bytes=64) for a in range(PASSES)]
+        g_codes = [keep.tile([P, SLOTS], U32, name=f"gcodes{a}", align_bytes=64) for a in range(PASSES)]
+        g_planes = [keep.tile([P, SLOTS], U8, name=f"gplanes{a}", align_bytes=64) for a in range(PASSES)]
+        raw = {}
+        grouped = {}
+        for a in range(PASSES):
+            for c, (t0, w, v) in enumerate(CHUNKS[a]):
+                raw[a, c] = keep.tile([P, PACK, w], F32, name=f"raw{a}_{c}")
+                grouped[a, c] = keep.tile([P, w, PACK], BF16, name=f"grouped{a}_{c}", align_bytes=64)
+
+        for a in range(PASSES):
+            nc.gpsimd.memset(planes[a][:].bitcast(I32), 0)
+        nc.gpsimd.memset(ws[:].rearrange("p x n -> p (x n)").bitcast(I32), 0)
+        for h in range(HALVES):
+            nc.gpsimd.memset(out_t[h][:], 0.0)
+
+        x_rows = xT.rearrange("(a p j) t -> a p j t", p=P, j=PACK)
+        for a in range(PASSES):
+            for c, (t0, w, v) in enumerate(CHUNKS[a]):
+                nc.sync.dma_start(raw[a, c][:], x_rows[a, :, :, t0 : t0 + w])
+            if a == 0:
+                nc.sync.dma_start(offs_t[:], offs)
+        s_rows = w_scales.rearrange("e a q n -> q (e a) n")
+        for q in range(4):
+            nc.sync.dma_start(
+                ws[32 * q : 32 * q + 4, :, :].bitcast(I32), s_rows[4 * q : 4 * q + 4, :, :].bitcast(I32)
+            )
+        w_rows = w_words.rearrange("e a p n -> p (e a) n")
+        for part in range(2):
+            x = slice(part * E * PASSES // 2, (part + 1) * E * PASSES // 2)
+            nc.sync.dma_start(ww[:, x, :].bitcast(I32), w_rows[:, x, :].bitcast(I32))
+            if part == 0:
+                nc.sync.dma_start(bias[:], b.rearrange("(h p) e -> p h e", p=P))
+                nc.sync.dma_start(dst_t[:], dst)
+                nc.sync.dma_start(gate_t[0][:], gate[0:P, :])
+        nc.sync.dma_start(gate_t[1][:], gate[P : 2 * P, :])
+
+        def scalar_copy(o, i):
+            nc.scalar.activation(o, i, COPY)
+
+        def gather(dst_tile, window, s):
+            nc.vector.tensor_copy(
+                dst_tile[:, s : s + PIECE], window[:].indirect(offs_t[:, s // 16 : (s + PIECE) // 16])
+            )
+
+        for a in range(PASSES):
+            for c, (t0, w, v) in enumerate(CHUNKS[a]):
+                if v > 0:
+                    interleave(nc.vector.tensor_copy, grouped[a, c], raw[a, c], 0, v)
+                interleave(scalar_copy, grouped[a, c], raw[a, c], v, w)
+                nc.vector.quantize_mx(
+                    out=codes[a][:, t0 : t0 + w].bitcast(FP8X4),
+                    scales=planes[a][:, t0 : t0 + w],
+                    in_=grouped[a, c][:].rearrange("p w j -> p (w j)"),
+                )
+            if a == 0:
+                gather(g_codes[0], codes[0], 0)
+                gather(g_codes[0], codes[0], PIECE)
+                gather(g_planes[0], planes[0], 0)
+            else:
+                gather(g_planes[0], planes[0], PIECE)
+                for s in range(0, SLOTS, PIECE):
+                    gather(g_codes[1], codes[1], s)
+                    gather(g_planes[1], planes[1], s)
+
+        y = {}
+        per = PIECE // C
+        for s in range(0, SLOTS, PIECE):
+            acc = {}
+            for a in range(PASSES):
+                for h in range(HALVES):
+                    for i in range(per):
+                        if a == 0:
+                            acc[h, i] = psum.tile([P, C], F32, name=f"acc{h}_{i}")
+                        e = s // C + i
+                        x = e * PASSES + a
+                        nc.tensor.matmul_mx(
+                            out=acc[h, i][:],
+                            lhsT=ww[:, x, h * 2 * P : (h + 1) * 2 * P].bitcast(FP4X4),
+                            lhsT_scale=ws[:, x, h * P : (h + 1) * P],
+                            rhs=g_codes[a][:, e * C : (e + 1) * C].bitcast(FP8X4),
+                            rhs_scale=g_planes[a][:, e * C : (e + 1) * C],
+                            start=(a == 0),
+                            stop=(a == PASSES - 1),
+                        )
+            for h in range(HALVES):
+                y[h, s] = keep.tile([P, PIECE], F32, name=f"y{h}_{s}")
+                for i in range(per):
+                    e = s // C + i
+                    nc.scalar.activation(
+                        y[h, s][:, i * C : (i + 1) * C], acc[h, i][:], RELU, bias=bias[:, h, e : e + 1]
+                    )
+        for s in range(0, SLOTS, PIECE):
+            for h in range(HALVES):
+                nc.vector.tensor_tensor(
+                    out_t[h][:].indirect(dst_t[:, s // 16 : (s + PIECE) // 16]),
+                    y[h, s][:],
+                    gate_t[h][:, s : s + PIECE],
+                    MULT,
+                )
+        for h in range(HALVES):
+            nc.sync.dma_start(out[h * P : (h + 1) * P, :], out_t[h][:])

@@ -23,8 +23,8 @@ RELU = mybir.ActivationFunctionType.Relu
 MULT = mybir.AluOpType.mult
 
 CHUNKS = (
-    ((0, 256, 160), (256, 512, 336), (768, 256, 192), (1024, 256, 192)),
-    ((0, 512, 0), (512, 512, 64), (1024, 256, 128)),
+    ((0, 512, 256), (512, 256, 128), (768, 256, 128), (1024, 128, 80), (1152, 128, 88)),
+    ((0, 256, 0), (256, 256, 0), (512, 256, 0), (768, 256, 0), (1024, 128, 0), (1152, 128, 0)),
 )
 PIECE = 512
 
@@ -46,7 +46,7 @@ def tile_moe_two_lin_relu_kernel(tc, xT, w_words, w_scales, b, gate, offs, dst, 
         dst_t = keep.tile([P, SLOTS // 16], U16, name="dst_t")
         ww = keep.tile([P, E * PASSES, 2 * N], U8, name="ww", align_bytes=64)
         ws = keep.tile([P, E * PASSES, N], U8, name="ws", align_bytes=64)
-        gate_t = [keep.tile([P, SLOTS], F32, name=f"gate{h}") for h in range(HALVES)]
+        gate_t = keep.tile([P, SLOTS], F32, name="gate_t")
         bias = keep.tile([P, HALVES, E], F32, name="bias")
         out_t = [keep.tile([P, T], F32, name=f"out{h}") for h in range(HALVES)]
         codes = [keep.tile([P, T], U32, name=f"codes{a}", align_bytes=64) for a in range(PASSES)]
@@ -61,8 +61,8 @@ def tile_moe_two_lin_relu_kernel(tc, xT, w_words, w_scales, b, gate, offs, dst, 
                 grouped[a, c] = keep.tile([P, w, PACK], BF16, name=f"grouped{a}_{c}", align_bytes=64)
 
         for a in range(PASSES):
-            nc.gpsimd.memset(planes[a][:].bitcast(I32), 0)
-        nc.gpsimd.memset(ws[:].rearrange("p x n -> p (x n)").bitcast(I32), 0)
+            nc.vector.memset(planes[a][:].bitcast(I32), 0)
+        nc.vector.memset(ws[:].rearrange("p x n -> p (x n)").bitcast(I32), 0)
         for h in range(HALVES):
             nc.gpsimd.memset(out_t[h][:], 0.0)
 
@@ -84,8 +84,7 @@ def tile_moe_two_lin_relu_kernel(tc, xT, w_words, w_scales, b, gate, offs, dst, 
             if part == 0:
                 nc.sync.dma_start(bias[:], b.rearrange("(h p) e -> p h e", p=P))
                 nc.sync.dma_start(dst_t[:], dst)
-                nc.sync.dma_start(gate_t[0][:], gate[0:P, :])
-        nc.sync.dma_start(gate_t[1][:], gate[P : 2 * P, :])
+                nc.sync.dma_start(gate_t[:], gate[0:P, :])
 
         def scalar_copy(o, i):
             nc.scalar.activation(o, i, COPY)
@@ -99,21 +98,16 @@ def tile_moe_two_lin_relu_kernel(tc, xT, w_words, w_scales, b, gate, offs, dst, 
             for c, (t0, w, v) in enumerate(CHUNKS[a]):
                 if v > 0:
                     interleave(nc.vector.tensor_copy, grouped[a, c], raw[a, c], 0, v)
-                interleave(scalar_copy, grouped[a, c], raw[a, c], v, w)
+                if v < w:
+                    interleave(scalar_copy, grouped[a, c], raw[a, c], v, w)
                 nc.vector.quantize_mx(
                     out=codes[a][:, t0 : t0 + w].bitcast(FP8X4),
                     scales=planes[a][:, t0 : t0 + w],
                     in_=grouped[a, c][:].rearrange("p w j -> p (w j)"),
                 )
-            if a == 0:
-                gather(g_codes[0], codes[0], 0)
-                gather(g_codes[0], codes[0], PIECE)
-                gather(g_planes[0], planes[0], 0)
-            else:
-                gather(g_planes[0], planes[0], PIECE)
-                for s in range(0, SLOTS, PIECE):
-                    gather(g_codes[1], codes[1], s)
-                    gather(g_planes[1], planes[1], s)
+            for s in range(0, SLOTS, PIECE):
+                gather(g_codes[a], codes[a], s)
+                gather(g_planes[a], planes[a], s)
 
         y = {}
         per = PIECE // C
@@ -147,7 +141,7 @@ def tile_moe_two_lin_relu_kernel(tc, xT, w_words, w_scales, b, gate, offs, dst, 
                 nc.vector.tensor_tensor(
                     out_t[h][:].indirect(dst_t[:, s // 16 : (s + PIECE) // 16]),
                     y[h, s][:],
-                    gate_t[h][:, s : s + PIECE],
+                    gate_t[:, s : s + PIECE],
                     MULT,
                 )
         for h in range(HALVES):

@@ -9,6 +9,10 @@ P = 128
 PACK = 4
 PASSES = K // (P * PACK)
 HALVES = N // P
+PIECE = 2 * C
+PIECES = SLOTS // PIECE
+FIRST = ((0, PIECE), (PIECE, 2 * PIECE), (2 * PIECE, SLOTS))
+AHEAD = 2
 
 F32 = mybir.dt.float32
 BF16 = mybir.dt.bfloat16
@@ -22,18 +26,7 @@ COPY = mybir.ActivationFunctionType.Copy
 RELU = mybir.ActivationFunctionType.Relu
 MULT = mybir.AluOpType.mult
 
-CHUNKS = (
-    ((0, 512, 256), (512, 256, 128), (768, 256, 128), (1024, 128, 80), (1152, 128, 88)),
-    ((0, 256, 0), (256, 256, 0), (512, 256, 0), (768, 256, 0), (1024, 128, 0), (1152, 128, 0)),
-)
-PIECE = 512
-
-
-def interleave(copy, grouped, raw, a, b):
-    copy(
-        grouped[:, a:b, :].rearrange("p (c i) t -> p c t i", i=4),
-        raw[:, :, a:b].rearrange("p t (c i) -> p c t i", i=4),
-    )
+LOADS = (((896, 576), (384, 256)), ((640, 0), (640, 224)))
 
 
 def tile_moe_two_lin_relu_kernel(tc, xT, w_words, w_scales, b, gate, offs, dst, out):
@@ -44,105 +37,172 @@ def tile_moe_two_lin_relu_kernel(tc, xT, w_words, w_scales, b, gate, offs, dst, 
 
         offs_t = keep.tile([P, SLOTS // 16], U16, name="offs_t")
         dst_t = keep.tile([P, SLOTS // 16], U16, name="dst_t")
-        ww = keep.tile([P, E * PASSES, 2 * N], U8, name="ww", align_bytes=64)
-        ws = keep.tile([P, E * PASSES, N], U8, name="ws", align_bytes=64)
+        ww = [keep.tile([P, 2 * PASSES, 2 * N], U8, name=f"ww{i}", align_bytes=64) for i in range(PIECES)]
+        ws_first = keep.tile([P, 2 * PASSES, N], U8, name="ws_first", align_bytes=64)
+        ws_rest = keep.tile([P, (E - 2) * PASSES, N], U8, name="ws_rest", align_bytes=64)
         gate_t = keep.tile([P, SLOTS], F32, name="gate_t")
-        bias = keep.tile([P, HALVES, E], F32, name="bias")
+        bias = keep.tile([P, HALVES, 2 * AHEAD], F32, name="bias")
         out_t = [keep.tile([P, T], F32, name=f"out{h}") for h in range(HALVES)]
-        codes = [keep.tile([P, T], U32, name=f"codes{a}", align_bytes=64) for a in range(PASSES)]
-        planes = [keep.tile([P, T], U8, name=f"planes{a}", align_bytes=64) for a in range(PASSES)]
-        g_codes = [keep.tile([P, SLOTS], U32, name=f"gcodes{a}", align_bytes=64) for a in range(PASSES)]
-        g_planes = [keep.tile([P, SLOTS], U8, name=f"gplanes{a}", align_bytes=64) for a in range(PASSES)]
-        raw = {}
-        grouped = {}
-        for a in range(PASSES):
-            for c, (t0, w, v) in enumerate(CHUNKS[a]):
-                raw[a, c] = keep.tile([P, PACK, w], F32, name=f"raw{a}_{c}")
-                grouped[a, c] = keep.tile([P, w, PACK], BF16, name=f"grouped{a}_{c}", align_bytes=64)
+        raw_pair = {
+            (u, c): keep.tile([P, 2, LOADS[u][c][0]], F32, name=f"rawpair{u}_{c}") for u in range(2) for c in range(2)
+        }
+        last = keep.tile([P, 8 * PIECE], F32, name="last", align_bytes=64)
+        raw_row = [keep.tile([P, T], F32, name=f"rawrow{j}", align_bytes=64)[:] for j in range(PACK - 1)]
+        raw_row.append(last[:, PIECE : PIECE + T])
+        win_pair = [keep.tile([P, T, 2], BF16, name=f"winpair{u}") for u in range(2)]
+        win_row = [keep.tile([P, T], BF16, name=f"winrow{j}") for j in range(PACK)]
+        pairs0 = {s0: keep.tile([P, 2, s1 - s0], U32, name=f"pairs0_{s0}") for s0, s1 in FIRST}
+        pairs1 = {i: keep.tile([P, 2, PIECE], U32, name=f"pairs1_{i}")[:] for i in range(PIECES) if i != 1}
+        pairs1[1] = last[:, 0 : 2 * PIECE].bitcast(U32).rearrange("p (u s) -> p u s", u=2)
+        codes0 = {s0: keep.tile([P, s1 - s0], U32, name=f"codes0_{s0}", align_bytes=64) for s0, s1 in FIRST[1:]}
+        planes0 = {s0: keep.tile([P, s1 - s0], U8, name=f"planes0_{s0}", align_bytes=64) for s0, s1 in FIRST}
+        codes1 = [keep.tile([P, PIECE], U32, name=f"codes1_{i}", align_bytes=64) for i in range(PIECES)]
+        planes1 = [keep.tile([P, PIECE], U8, name=f"planes1_{i}", align_bytes=64) for i in range(PIECES)]
 
-        for a in range(PASSES):
-            nc.vector.memset(planes[a][:].bitcast(I32), 0)
-        nc.vector.memset(ws[:].rearrange("p x n -> p (x n)").bitcast(I32), 0)
+        nc.vector.memset(ws_first[:].rearrange("p x n -> p (x n)").bitcast(I32), 0)
+        nc.vector.memset(ws_rest[:].rearrange("p x n -> p (x n)").bitcast(I32), 0)
         for h in range(HALVES):
             nc.gpsimd.memset(out_t[h][:], 0.0)
 
-        x_rows = xT.rearrange("(a p j) t -> a p j t", p=P, j=PACK)
-        for a in range(PASSES):
-            for c, (t0, w, v) in enumerate(CHUNKS[a]):
-                nc.sync.dma_start(raw[a, c][:], x_rows[a, :, :, t0 : t0 + w])
-            if a == 0:
-                nc.sync.dma_start(offs_t[:], offs)
-        s_rows = w_scales.rearrange("e a q n -> q (e a) n")
-        for q in range(4):
-            nc.sync.dma_start(
-                ws[32 * q : 32 * q + 4, :, :].bitcast(I32), s_rows[4 * q : 4 * q + 4, :, :].bitcast(I32)
-            )
-        w_rows = w_words.rearrange("e a p n -> p (e a) n")
-        for part in range(2):
-            x = slice(part * E * PASSES // 2, (part + 1) * E * PASSES // 2)
-            nc.sync.dma_start(ww[:, x, :].bitcast(I32), w_rows[:, x, :].bitcast(I32))
-            if part == 0:
-                nc.sync.dma_start(bias[:], b.rearrange("(h p) e -> p h e", p=P))
-                nc.sync.dma_start(dst_t[:], dst)
-                nc.sync.dma_start(gate_t[:], gate[0:P, :])
+        def bias_of(h, i):
+            if i + AHEAD < PIECES:
+                return pairs1[i + AHEAD][:, h, 0:2].bitcast(F32)
+            return bias[:, h, 2 * (i + AHEAD - PIECES) : 2 * (i + AHEAD - PIECES) + 2]
 
-        def scalar_copy(o, i):
+        x_rows = xT.rearrange("(a p j) t -> a p j t", p=P, j=PACK)
+        for u in range(2):
+            for c in range(2):
+                t0 = c * LOADS[u][0][0]
+                nc.sync.dma_start(raw_pair[u, c][:], x_rows[0, :, 2 * u : 2 * u + 2, t0 : t0 + LOADS[u][c][0]])
+            if u == 0:
+                nc.sync.dma_start(offs_t[:], offs)
+        for j in range(PACK):
+            nc.sync.dma_start(raw_row[j], x_rows[1, :, j, :])
+
+        s_rows = w_scales.rearrange("e a q n -> q (e a) n")
+        b_rows = b.rearrange("(h p) e -> p h e", p=P)
+        w_rows = w_words.rearrange("e a p n -> p (e a) n")
+
+        def load_scales(ws, x0, x1):
+            for q in range(4):
+                nc.sync.dma_start(
+                    ws[32 * q : 32 * q + 4, :, :].bitcast(I32), s_rows[4 * q : 4 * q + 4, x0:x1, :].bitcast(I32)
+                )
+
+        for i in range(PIECES):
+            nc.sync.dma_start(ww[i][:].bitcast(I32), w_rows[:, 2 * PASSES * i : 2 * PASSES * (i + 1), :].bitcast(I32))
+            if i == 0:
+                load_scales(ws_first, 0, 2 * PASSES)
+            if i == 1:
+                load_scales(ws_rest, 2 * PASSES, E * PASSES)
+            if i + AHEAD < PIECES:
+                for h in range(HALVES):
+                    nc.sync.dma_start(bias_of(h, i), b_rows[:, h, 2 * i : 2 * i + 2])
+            if i + AHEAD == PIECES:
+                nc.sync.dma_start(bias[:], b_rows[:, :, 2 * i :])
+            if i == 0:
+                nc.sync.dma_start(dst_t[:], dst)
+            nc.sync.dma_start(gate_t[:, i * PIECE : (i + 1) * PIECE], gate[0:P, i * PIECE : (i + 1) * PIECE])
+
+        def scalar_cast(o, i):
             nc.scalar.activation(o, i, COPY)
 
-        def gather(dst_tile, window, s):
-            nc.vector.tensor_copy(
-                dst_tile[:, s : s + PIECE], window[:].indirect(offs_t[:, s // 16 : (s + PIECE) // 16])
+        def slots(listed, s0, s1):
+            return listed[:, s0 // 16 : s1 // 16]
+
+        def interleave(copy, u, c, t0, t1):
+            first = c * LOADS[u][0][0]
+            copy(
+                win_pair[u][:, first + t0 : first + t1, :].rearrange("p (c i) e -> p c e i", i=4),
+                raw_pair[u, c][:, :, t0:t1].rearrange("p e (c i) -> p c e i", i=4),
             )
 
-        for a in range(PASSES):
-            for c, (t0, w, v) in enumerate(CHUNKS[a]):
+        for u in range(2):
+            for c in range(2):
+                n, v = LOADS[u][c]
                 if v > 0:
-                    interleave(nc.vector.tensor_copy, grouped[a, c], raw[a, c], 0, v)
-                if v < w:
-                    interleave(scalar_copy, grouped[a, c], raw[a, c], v, w)
-                nc.vector.quantize_mx(
-                    out=codes[a][:, t0 : t0 + w].bitcast(FP8X4),
-                    scales=planes[a][:, t0 : t0 + w],
-                    in_=grouped[a, c][:].rearrange("p w j -> p (w j)"),
-                )
-            for s in range(0, SLOTS, PIECE):
-                gather(g_codes[a], codes[a], s)
-                gather(g_planes[a], planes[a], s)
+                    interleave(nc.vector.tensor_copy, u, c, 0, v)
+                interleave(scalar_cast, u, c, v, n)
+            window = win_pair[u][:].rearrange("p t e -> p (t e)").bitcast(U32)
+            for s0, s1 in FIRST:
+                nc.vector.tensor_copy(pairs0[s0][:, u, :], window.indirect(slots(offs_t, s0, s1)))
 
-        y = {}
-        per = PIECE // C
-        for s in range(0, SLOTS, PIECE):
+        for j in range(PACK):
+            cast = scalar_cast if j == 0 else nc.vector.tensor_copy
+            cast(win_row[j][:], raw_row[j])
+
+        def gather_pair(u, i):
+            for e in range(2):
+                into = pairs1[i][:, u, :].bitcast(BF16).rearrange("p (s e) -> p s e", e=2)[:, :, e]
+                nc.scalar.activation(into, win_row[2 * u + e][:].indirect(slots(offs_t, i * PIECE, (i + 1) * PIECE)), COPY)
+
+        def merge(copy, word, quads, pairs):
+            copy(
+                quads.bitcast(word).rearrange("p (c i u) -> p c u i", i=4, u=2),
+                pairs.bitcast(word).rearrange("p u (c i) -> p c u i", i=4),
+            )
+
+        def quantise(codes, planes, quads):
+            nc.vector.quantize_mx(out=codes[:].bitcast(FP8X4), scales=planes[:], in_=quads)
+
+        def finish(i):
+            quads = keep.tile([P, PIECE * PACK], BF16, name=f"quads1_{i}", align_bytes=64)
+            copy, word = (nc.vector.tensor_copy, I32) if i < PIECES - 1 else (nc.scalar.copy, U32)
+            merge(copy, word, quads[:], pairs1[i])
+            quantise(codes1[i], planes1[i], quads[:])
+
+        for u in range(2):
+            for i in range(AHEAD):
+                gather_pair(u, i)
+        quads_a = keep.tile([P, PIECE * PACK], BF16, name="quads_a", align_bytes=64)
+        codes0[0] = keep.tile([P, PIECE], U32, name="rawrow1", align_bytes=64)
+        quads_b = last[:, 2 * PIECE : 4 * PIECE].bitcast(BF16)
+        quads_c = last[:, 4 * PIECE : 8 * PIECE].bitcast(BF16)
+        merge(nc.vector.tensor_copy, I32, quads_a[:], pairs0[0][:])
+        quantise(codes0[0], planes0[0], quads_a[:])
+        merge(nc.vector.tensor_copy, I32, quads_b, pairs0[PIECE][:])
+        merge(nc.vector.tensor_copy, I32, quads_c, pairs0[2 * PIECE][:])
+        finish(0)
+        quantise(codes0[PIECE], planes0[PIECE], quads_b)
+        quantise(codes0[2 * PIECE], planes0[2 * PIECE], quads_c)
+        finish(1)
+
+        turn = 0
+        for i in range(PIECES):
             acc = {}
+            g0 = max(s0 for s0, s1 in FIRST if s0 <= i * PIECE)
             for a in range(PASSES):
                 for h in range(HALVES):
-                    for i in range(per):
+                    for e in range(2):
                         if a == 0:
-                            acc[h, i] = psum.tile([P, C], F32, name=f"acc{h}_{i}")
-                        e = s // C + i
-                        x = e * PASSES + a
+                            acc[h, e] = psum.tile([P, C], F32, name=f"acc{turn % 8}")
+                            turn = turn + 1
+                        ws = ws_first[:, e * PASSES + a, :] if i == 0 else ws_rest[:, (2 * i + e - 2) * PASSES + a, :]
+                        c0 = e * C + (i * PIECE - g0 if a == 0 else 0)
                         nc.tensor.matmul_mx(
-                            out=acc[h, i][:],
-                            lhsT=ww[:, x, h * 2 * P : (h + 1) * 2 * P].bitcast(FP4X4),
-                            lhsT_scale=ws[:, x, h * P : (h + 1) * P],
-                            rhs=g_codes[a][:, e * C : (e + 1) * C].bitcast(FP8X4),
-                            rhs_scale=g_planes[a][:, e * C : (e + 1) * C],
+                            out=acc[h, e][:],
+                            lhsT=ww[i][:, e * PASSES + a, h * 2 * P : (h + 1) * 2 * P].bitcast(FP4X4),
+                            lhsT_scale=ws[:, h * P : (h + 1) * P],
+                            rhs=(codes0[g0], codes1[i])[a][:, c0 : c0 + C].bitcast(FP8X4),
+                            rhs_scale=(planes0[g0], planes1[i])[a][:, c0 : c0 + C],
                             start=(a == 0),
                             stop=(a == PASSES - 1),
                         )
             for h in range(HALVES):
-                y[h, s] = keep.tile([P, PIECE], F32, name=f"y{h}_{s}")
-                for i in range(per):
-                    e = s // C + i
+                y = keep.tile([P, PIECE], F32, name=f"y{h}_{i}")
+                for e in range(2):
                     nc.scalar.activation(
-                        y[h, s][:, i * C : (i + 1) * C], acc[h, i][:], RELU, bias=bias[:, h, e : e + 1]
+                        y[:, e * C : (e + 1) * C], acc[h, e][:], RELU, bias=bias_of(h, i)[:, e : e + 1]
                     )
-        for s in range(0, SLOTS, PIECE):
-            for h in range(HALVES):
                 nc.vector.tensor_tensor(
-                    out_t[h][:].indirect(dst_t[:, s // 16 : (s + PIECE) // 16]),
-                    y[h, s][:],
-                    gate_t[:, s : s + PIECE],
+                    out_t[h][:].indirect(slots(dst_t, i * PIECE, (i + 1) * PIECE)),
+                    y[:],
+                    gate_t[:, i * PIECE : (i + 1) * PIECE],
                     MULT,
                 )
+                if i + AHEAD < PIECES:
+                    gather_pair(h, i + AHEAD)
+            if i + AHEAD < PIECES:
+                finish(i + AHEAD)
         for h in range(HALVES):
             nc.sync.dma_start(out[h * P : (h + 1) * P, :], out_t[h][:])

@@ -27,6 +27,7 @@ RELU = mybir.ActivationFunctionType.Relu
 MULT = mybir.AluOpType.mult
 
 LOADS = (((896, 576), (384, 256)), ((640, 0), (640, 224)))
+ROW_SHARES = (0, 832, T, T)
 
 
 def tile_moe_two_lin_relu_kernel(tc, xT, w_words, w_scales, b, gate, offs, dst, out):
@@ -37,7 +38,7 @@ def tile_moe_two_lin_relu_kernel(tc, xT, w_words, w_scales, b, gate, offs, dst, 
 
         offs_t = keep.tile([P, SLOTS // 16], U16, name="offs_t")
         dst_t = keep.tile([P, SLOTS // 16], U16, name="dst_t")
-        ww = [keep.tile([P, 2 * PASSES, 2 * N], U8, name=f"ww{i}", align_bytes=64) for i in range(PIECES)]
+        ww = [keep.tile([P, (s1 - s0) // C * PASSES, 2 * N], U8, name=f"ww{s0}", align_bytes=64) for s0, s1 in FIRST]
         ws_first = keep.tile([P, 2 * PASSES, N], U8, name="ws_first", align_bytes=64)
         ws_rest = keep.tile([P, (E - 2) * PASSES, N], U8, name="ws_rest", align_bytes=64)
         gate_t = keep.tile([P, SLOTS], F32, name="gate_t")
@@ -89,20 +90,23 @@ def tile_moe_two_lin_relu_kernel(tc, xT, w_words, w_scales, b, gate, offs, dst, 
                     ws[32 * q : 32 * q + 4, :, :].bitcast(I32), s_rows[4 * q : 4 * q + 4, x0:x1, :].bitcast(I32)
                 )
 
-        for i in range(PIECES):
-            nc.sync.dma_start(ww[i][:].bitcast(I32), w_rows[:, 2 * PASSES * i : 2 * PASSES * (i + 1), :].bitcast(I32))
-            if i == 0:
-                load_scales(ws_first, 0, 2 * PASSES)
-            if i == 1:
-                load_scales(ws_rest, 2 * PASSES, E * PASSES)
-            if i + AHEAD < PIECES:
-                for h in range(HALVES):
-                    nc.sync.dma_start(bias_of(h, i), b_rows[:, h, 2 * i : 2 * i + 2])
-            if i + AHEAD == PIECES:
-                nc.sync.dma_start(bias[:], b_rows[:, :, 2 * i :])
-            if i == 0:
-                nc.sync.dma_start(dst_t[:], dst)
-            nc.sync.dma_start(gate_t[:, i * PIECE : (i + 1) * PIECE], gate[0:P, i * PIECE : (i + 1) * PIECE])
+        def load_words(ww, i0, i1):
+            nc.sync.dma_start(ww[:].bitcast(I32), w_rows[:, 2 * PASSES * i0 : 2 * PASSES * i1, :].bitcast(I32))
+
+        def load_bias(i):
+            nc.sync.dma_start(pairs1[i + AHEAD][:, :, 0:2].bitcast(F32), b_rows[:, :, 2 * i : 2 * i + 2])
+
+        load_words(ww[0], 0, 1)
+        load_scales(ws_first, 0, 2 * PASSES)
+        load_bias(0)
+        nc.sync.dma_start(dst_t[:], dst)
+        nc.sync.dma_start(gate_t[:, 0:PIECE], gate[0:P, 0:PIECE])
+        load_words(ww[1], 1, 2)
+        load_scales(ws_rest, 2 * PASSES, E * PASSES)
+        load_bias(1)
+        nc.sync.dma_start(gate_t[:, PIECE:], gate[0:P, PIECE:])
+        load_words(ww[2], 2, PIECES)
+        nc.sync.dma_start(bias[:], b_rows[:, :, 2 * (PIECES - AHEAD) :])
 
         def scalar_cast(o, i):
             nc.scalar.activation(o, i, COPY)
@@ -128,8 +132,11 @@ def tile_moe_two_lin_relu_kernel(tc, xT, w_words, w_scales, b, gate, offs, dst, 
                 nc.vector.tensor_copy(pairs0[s0][:, u, :], window.indirect(slots(offs_t, s0, s1)))
 
         for j in range(PACK):
-            cast = scalar_cast if j == 0 else nc.vector.tensor_copy
-            cast(win_row[j][:], raw_row[j])
+            v = ROW_SHARES[j]
+            if v > 0:
+                nc.vector.tensor_copy(win_row[j][:, 0:v], raw_row[j][:, 0:v])
+            if v < T:
+                scalar_cast(win_row[j][:, v:T], raw_row[j][:, v:T])
 
         def gather_pair(u, i):
             for e in range(2):
@@ -154,8 +161,8 @@ def tile_moe_two_lin_relu_kernel(tc, xT, w_words, w_scales, b, gate, offs, dst, 
         for u in range(2):
             for i in range(AHEAD):
                 gather_pair(u, i)
-        quads_a = keep.tile([P, PIECE * PACK], BF16, name="quads_a", align_bytes=64)
-        codes0[0] = keep.tile([P, PIECE], U32, name="rawrow1", align_bytes=64)
+        quads_a = keep.tile([P, PIECE * PACK], BF16, name="rawrow1", align_bytes=64)
+        codes0[0] = keep.tile([P, PIECE], U32, name="rawrow2", align_bytes=64)
         quads_b = last[:, 2 * PIECE : 4 * PIECE].bitcast(BF16)
         quads_c = last[:, 4 * PIECE : 8 * PIECE].bitcast(BF16)
         merge(nc.vector.tensor_copy, I32, quads_a[:], pairs0[0][:])
@@ -167,7 +174,6 @@ def tile_moe_two_lin_relu_kernel(tc, xT, w_words, w_scales, b, gate, offs, dst, 
         quantise(codes0[2 * PIECE], planes0[2 * PIECE], quads_c)
         finish(1)
 
-        turn = 0
         for i in range(PIECES):
             acc = {}
             g0 = max(s0 for s0, s1 in FIRST if s0 <= i * PIECE)
@@ -175,13 +181,12 @@ def tile_moe_two_lin_relu_kernel(tc, xT, w_words, w_scales, b, gate, offs, dst, 
                 for h in range(HALVES):
                     for e in range(2):
                         if a == 0:
-                            acc[h, e] = psum.tile([P, C], F32, name=f"acc{turn % 8}")
-                            turn = turn + 1
+                            acc[h, e] = psum.tile([P, C], F32, name=f"acc{h}_{e}")
                         ws = ws_first[:, e * PASSES + a, :] if i == 0 else ws_rest[:, (2 * i + e - 2) * PASSES + a, :]
                         c0 = e * C + (i * PIECE - g0 if a == 0 else 0)
                         nc.tensor.matmul_mx(
                             out=acc[h, e][:],
-                            lhsT=ww[i][:, e * PASSES + a, h * 2 * P : (h + 1) * 2 * P].bitcast(FP4X4),
+                            lhsT=ww[g0 // PIECE][:, (2 * i + e - g0 // C) * PASSES + a, h * 2 * P : (h + 1) * 2 * P].bitcast(FP4X4),
                             lhsT_scale=ws[:, h * P : (h + 1) * P],
                             rhs=(codes0[g0], codes1[i])[a][:, c0 : c0 + C].bitcast(FP8X4),
                             rhs_scale=(planes0[g0], planes1[i])[a][:, c0 : c0 + C],

@@ -27,7 +27,7 @@ RELU = mybir.ActivationFunctionType.Relu
 MULT = mybir.AluOpType.mult
 
 LOADS = (((896, 576), (384, 256)), ((640, 0), (640, 224)))
-ROW_SHARES = (0, 832, T, T)
+ROW_SHARES = (0, T, T, T)
 
 
 def tile_moe_two_lin_relu_kernel(tc, xT, w_words, w_scales, b, gate, offs, dst, out):
@@ -161,8 +161,8 @@ def tile_moe_two_lin_relu_kernel(tc, xT, w_words, w_scales, b, gate, offs, dst, 
         for u in range(2):
             for i in range(AHEAD):
                 gather_pair(u, i)
-        quads_a = keep.tile([P, PIECE * PACK], BF16, name="rawrow1", align_bytes=64)
-        codes0[0] = keep.tile([P, PIECE], U32, name="rawrow2", align_bytes=64)
+        quads_a = keep.tile([P, PIECE * PACK], BF16, name="quads_a", align_bytes=64)
+        codes0[0] = keep.tile([P, PIECE], U32, name="rawrow1", align_bytes=64)
         quads_b = last[:, 2 * PIECE : 4 * PIECE].bitcast(BF16)
         quads_c = last[:, 4 * PIECE : 8 * PIECE].bitcast(BF16)
         merge(nc.vector.tensor_copy, I32, quads_a[:], pairs0[0][:])

@@ -13,6 +13,7 @@ PIECE = 2 * C
 PIECES = SLOTS // PIECE
 FIRST = ((0, PIECE), (PIECE, 2 * PIECE), (2 * PIECE, SLOTS))
 AHEAD = 2
+TAIL = 384
 
 F32 = mybir.dt.float32
 BF16 = mybir.dt.bfloat16
@@ -26,8 +27,7 @@ COPY = mybir.ActivationFunctionType.Copy
 RELU = mybir.ActivationFunctionType.Relu
 MULT = mybir.AluOpType.mult
 
-LOADS = (((896, 576), (384, 256)), ((640, 0), (640, 224)))
-ROW_SHARES = (0, T, T, T)
+LOADS = (((896, 576), (384, 256)), ((640, 0), (640, 352)))
 
 
 def tile_moe_two_lin_relu_kernel(tc, xT, w_words, w_scales, b, gate, offs, dst, out):
@@ -47,14 +47,15 @@ def tile_moe_two_lin_relu_kernel(tc, xT, w_words, w_scales, b, gate, offs, dst, 
         raw_pair = {
             (u, c): keep.tile([P, 2, LOADS[u][c][0]], F32, name=f"rawpair{u}_{c}") for u in range(2) for c in range(2)
         }
-        last = keep.tile([P, 8 * PIECE], F32, name="last", align_bytes=64)
+        last = keep.tile([P, 10 * PIECE], F32, name="last", align_bytes=64)
+        raw_tail = last[:, 5 * PIECE - 64 : 5 * PIECE - 64 + TAIL]
         raw_row = [keep.tile([P, T], F32, name=f"rawrow{j}", align_bytes=64)[:] for j in range(PACK - 1)]
-        raw_row.append(last[:, PIECE : PIECE + T])
+        raw_row.append(keep.tile([P, T - TAIL], F32, name="rawrow3")[:])
         win_pair = [keep.tile([P, T, 2], BF16, name=f"winpair{u}") for u in range(2)]
         win_row = [keep.tile([P, T], BF16, name=f"winrow{j}") for j in range(PACK)]
         pairs0 = {s0: keep.tile([P, 2, s1 - s0], U32, name=f"pairs0_{s0}") for s0, s1 in FIRST}
         pairs1 = {i: keep.tile([P, 2, PIECE], U32, name=f"pairs1_{i}")[:] for i in range(PIECES) if i != 1}
-        pairs1[1] = last[:, 0 : 2 * PIECE].bitcast(U32).rearrange("p (u s) -> p u s", u=2)
+        pairs1[1] = last[:].bitcast(U32).rearrange("p (u s) -> p u s", u=2)[:, :, 0:PIECE]
         codes0 = {s0: keep.tile([P, s1 - s0], U32, name=f"codes0_{s0}", align_bytes=64) for s0, s1 in FIRST[1:]}
         planes0 = {s0: keep.tile([P, s1 - s0], U8, name=f"planes0_{s0}", align_bytes=64) for s0, s1 in FIRST}
         codes1 = [keep.tile([P, PIECE], U32, name=f"codes1_{i}", align_bytes=64) for i in range(PIECES)]
@@ -77,8 +78,10 @@ def tile_moe_two_lin_relu_kernel(tc, xT, w_words, w_scales, b, gate, offs, dst, 
                 nc.sync.dma_start(raw_pair[u, c][:], x_rows[0, :, 2 * u : 2 * u + 2, t0 : t0 + LOADS[u][c][0]])
             if u == 0:
                 nc.sync.dma_start(offs_t[:], offs)
-        for j in range(PACK):
+        for j in range(PACK - 1):
             nc.sync.dma_start(raw_row[j], x_rows[1, :, j, :])
+        nc.sync.dma_start(raw_row[3], x_rows[1, :, 3, 0 : T - TAIL])
+        nc.sync.dma_start(raw_tail, x_rows[1, :, 3, T - TAIL :])
 
         s_rows = w_scales.rearrange("e a q n -> q (e a) n")
         b_rows = b.rearrange("(h p) e -> p h e", p=P)
@@ -131,12 +134,11 @@ def tile_moe_two_lin_relu_kernel(tc, xT, w_words, w_scales, b, gate, offs, dst, 
             for s0, s1 in FIRST:
                 nc.vector.tensor_copy(pairs0[s0][:, u, :], window.indirect(slots(offs_t, s0, s1)))
 
-        for j in range(PACK):
-            v = ROW_SHARES[j]
-            if v > 0:
-                nc.vector.tensor_copy(win_row[j][:, 0:v], raw_row[j][:, 0:v])
-            if v < T:
-                scalar_cast(win_row[j][:, v:T], raw_row[j][:, v:T])
+        scalar_cast(win_row[0][:], raw_row[0])
+        for j in (1, 2):
+            nc.vector.tensor_copy(win_row[j][:], raw_row[j])
+        nc.vector.tensor_copy(win_row[3][:, 0 : T - TAIL], raw_row[3])
+        nc.vector.tensor_copy(win_row[3][:, T - TAIL :], raw_tail)
 
         def gather_pair(u, i):
             for e in range(2):
@@ -161,12 +163,12 @@ def tile_moe_two_lin_relu_kernel(tc, xT, w_words, w_scales, b, gate, offs, dst, 
         for u in range(2):
             for i in range(AHEAD):
                 gather_pair(u, i)
-        quads_a = keep.tile([P, PIECE * PACK], BF16, name="quads_a", align_bytes=64)
-        codes0[0] = keep.tile([P, PIECE], U32, name="rawrow1", align_bytes=64)
-        quads_b = last[:, 2 * PIECE : 4 * PIECE].bitcast(BF16)
-        quads_c = last[:, 4 * PIECE : 8 * PIECE].bitcast(BF16)
-        merge(nc.vector.tensor_copy, I32, quads_a[:], pairs0[0][:])
-        quantise(codes0[0], planes0[0], quads_a[:])
+        quads_a = raw_row[0][:, 0 : 2 * PIECE].bitcast(BF16)
+        codes0[0] = keep.tile([P, PIECE], U32, name="rawrow2", align_bytes=64)
+        quads_b = last[:, 6 * PIECE : 8 * PIECE].bitcast(BF16)
+        quads_c = last[:, PIECE : 5 * PIECE].bitcast(BF16)
+        merge(nc.vector.tensor_copy, I32, quads_a, pairs0[0][:])
+        quantise(codes0[0], planes0[0], quads_a)
         merge(nc.vector.tensor_copy, I32, quads_b, pairs0[PIECE][:])
         merge(nc.vector.tensor_copy, I32, quads_c, pairs0[2 * PIECE][:])
         finish(0)

@@ -120,8 +120,8 @@ def tile_moe_two_lin_relu_kernel(tc, xT, w_words, w_scales, b, gate, offs, dst, 
         def interleave(copy, u, c, t0, t1):
             first = c * LOADS[u][0][0]
             copy(
-                win_pair[u][:, first + t0 : first + t1, :].rearrange("p (c i) e -> p c e i", i=4),
-                raw_pair[u, c][:, :, t0:t1].rearrange("p e (c i) -> p c e i", i=4),
+                win_pair[u][:, first + t0 : first + t1, :],
+                raw_pair[u, c][:, :, t0:t1].rearrange("p e t -> p t e"),
             )
 
         for u in range(2):
@@ -147,8 +147,8 @@ def tile_moe_two_lin_relu_kernel(tc, xT, w_words, w_scales, b, gate, offs, dst, 
 
         def merge(copy, word, quads, pairs):
             copy(
-                quads.bitcast(word).rearrange("p (c i u) -> p c u i", i=4, u=2),
-                pairs.bitcast(word).rearrange("p u (c i) -> p c u i", i=4),
+                quads.bitcast(word).rearrange("p (s u) -> p s u", u=2),
+                pairs.bitcast(word).rearrange("p u s -> p s u"),
             )
 
         def quantise(codes, planes, quads):

@@ -11,9 +11,10 @@ PASSES = K // (P * PACK)
 HALVES = N // P
 PIECE = 2 * C
 PIECES = SLOTS // PIECE
-FIRST = ((0, PIECE), (PIECE, 2 * PIECE), (2 * PIECE, SLOTS))
-AHEAD = 2
+WIDE = 2 * PIECE
 TAIL = 384
+PLACES = ((5, 6), (0, 4), (1, 7))
+WEIGHTS = ((0, 1), (1, 2), (2, PIECES))
 
 F32 = mybir.dt.float32
 BF16 = mybir.dt.bfloat16
@@ -27,7 +28,8 @@ COPY = mybir.ActivationFunctionType.Copy
 RELU = mybir.ActivationFunctionType.Relu
 MULT = mybir.AluOpType.mult
 
-LOADS = (((896, 576), (384, 256)), ((640, 0), (640, 352)))
+LOADS = (((896, 576), (384, 256)), ((640, 0), (640, 416)), ((640, 0), (640, 352)))
+PAIRS = ((0, 0), (0, 2), (1, 2))
 
 
 def tile_moe_two_lin_relu_kernel(tc, xT, w_words, w_scales, b, gate, offs, dst, out):
@@ -38,26 +40,39 @@ def tile_moe_two_lin_relu_kernel(tc, xT, w_words, w_scales, b, gate, offs, dst, 
 
         offs_t = keep.tile([P, SLOTS // 16], U16, name="offs_t")
         dst_t = keep.tile([P, SLOTS // 16], U16, name="dst_t")
-        ww = [keep.tile([P, (s1 - s0) // C * PASSES, 2 * N], U8, name=f"ww{s0}", align_bytes=64) for s0, s1 in FIRST]
+        ww = [keep.tile([P, 2 * (i1 - i0) * PASSES, 2 * N], U8, name=f"ww{i0}", align_bytes=64) for i0, i1 in WEIGHTS]
         ws_first = keep.tile([P, 2 * PASSES, N], U8, name="ws_first", align_bytes=64)
         ws_rest = keep.tile([P, (E - 2) * PASSES, N], U8, name="ws_rest", align_bytes=64)
         gate_t = keep.tile([P, SLOTS], F32, name="gate_t")
-        bias = keep.tile([P, HALVES, 2 * AHEAD], F32, name="bias")
         out_t = [keep.tile([P, T], F32, name=f"out{h}") for h in range(HALVES)]
+
+        quads0 = keep.tile([P, 2 * SLOTS], F32, name="quads0", align_bytes=64)
+        shared = keep.tile([P, 13 * PIECE], F32, name="shared", align_bytes=64)
+
+        def unit(n, count=1):
+            return shared[:, n * PIECE : (n + count) * PIECE]
+
+        quads1_rest = keep.tile([P, PIECES, 2 * PIECE], F32, name="quads1_rest", align_bytes=64)
+        quads1 = [unit(7, 2)] + [quads1_rest[:, i, :] for i in range(PIECES - 1)]
+        pairs0 = keep.tile([P, 2, SLOTS], U32, name="pairs0")
+        pairs1 = [keep.tile([P, 2, PIECE], U32, name="pairs1_first", align_bytes=64)[:]]
+        for rows, words in PLACES:
+            both = unit(rows, 2 * (words - rows))
+            pairs1.append(both.bitcast(U32).rearrange("p (u s) -> p u s", u=2)[:, :, 0:PIECE])
+
         raw_pair = {
-            (u, c): keep.tile([P, 2, LOADS[u][c][0]], F32, name=f"rawpair{u}_{c}") for u in range(2) for c in range(2)
+            (u, c): keep.tile([P, 2, LOADS[u][c][0]], F32, name=f"rawpair{u}_{c}")[:]
+            for u in range(3)
+            for c in range(2)
+            if (u, c) != (2, 1)
         }
-        last = keep.tile([P, 10 * PIECE], F32, name="last", align_bytes=64)
-        raw_tail = last[:, 5 * PIECE - 64 : 5 * PIECE - 64 + TAIL]
-        raw_row = [keep.tile([P, T], F32, name=f"rawrow{j}", align_bytes=64)[:] for j in range(PACK - 1)]
-        raw_row.append(keep.tile([P, T - TAIL], F32, name="rawrow3")[:])
-        win_pair = [keep.tile([P, T, 2], BF16, name=f"winpair{u}") for u in range(2)]
-        win_row = [keep.tile([P, T], BF16, name=f"winrow{j}") for j in range(PACK)]
-        pairs0 = {s0: keep.tile([P, 2, s1 - s0], U32, name=f"pairs0_{s0}") for s0, s1 in FIRST}
-        pairs1 = {i: keep.tile([P, 2, PIECE], U32, name=f"pairs1_{i}")[:] for i in range(PIECES) if i != 1}
-        pairs1[1] = last[:].bitcast(U32).rearrange("p (u s) -> p u s", u=2)[:, :, 0:PIECE]
-        codes0 = {s0: keep.tile([P, s1 - s0], U32, name=f"codes0_{s0}", align_bytes=64) for s0, s1 in FIRST[1:]}
-        planes0 = {s0: keep.tile([P, s1 - s0], U8, name=f"planes0_{s0}", align_bytes=64) for s0, s1 in FIRST}
+        raw_pair[2, 1] = quads0[:, 0 : 2 * LOADS[2][1][0]].rearrange("p (e t) -> p e t", e=2)
+        raw_c = keep.tile([P, T], F32, name="raw_c")
+        raw_d = keep.tile([P, T - TAIL], F32, name="raw_d", align_bytes=64)[:]
+        raw_tail = shared[:, 5 * PIECE - TAIL // 2 : 5 * PIECE + TAIL // 2]
+        win_pair = [keep.tile([P, T, 2], BF16, name=f"winpair{u}") for u in range(3)]
+        win_row = [keep.tile([P, T], BF16, name=f"winrow{j}") for j in range(2)]
+        planes0 = [keep.tile([P, WIDE], U8, name=f"planes0_{g}", align_bytes=64) for g in range(2)]
         codes1 = [keep.tile([P, PIECE], U32, name=f"codes1_{i}", align_bytes=64) for i in range(PIECES)]
         planes1 = [keep.tile([P, PIECE], U8, name=f"planes1_{i}", align_bytes=64) for i in range(PIECES)]
 
@@ -67,24 +82,23 @@ def tile_moe_two_lin_relu_kernel(tc, xT, w_words, w_scales, b, gate, offs, dst, 
             nc.gpsimd.memset(out_t[h][:], 0.0)
 
         def bias_of(h, i):
-            if i + AHEAD < PIECES:
-                return pairs1[i + AHEAD][:, h, 0:2].bitcast(F32)
-            return bias[:, h, 2 * (i + AHEAD - PIECES) : 2 * (i + AHEAD - PIECES) + 2]
+            if h == 0:
+                return quads1_rest[:, i, 0:2]
+            return unit(i)[:, 0:2]
 
         x_rows = xT.rearrange("(a p j) t -> a p j t", p=P, j=PACK)
-        for u in range(2):
+        for u, (a, j) in enumerate(PAIRS):
             for c in range(2):
                 t0 = c * LOADS[u][0][0]
-                nc.sync.dma_start(raw_pair[u, c][:], x_rows[0, :, 2 * u : 2 * u + 2, t0 : t0 + LOADS[u][c][0]])
+                nc.sync.dma_start(raw_pair[u, c], x_rows[a, :, j : j + 2, t0 : t0 + LOADS[u][c][0]])
             if u == 0:
                 nc.sync.dma_start(offs_t[:], offs)
-        for j in range(PACK - 1):
-            nc.sync.dma_start(raw_row[j], x_rows[1, :, j, :])
-        nc.sync.dma_start(raw_row[3], x_rows[1, :, 3, 0 : T - TAIL])
-        nc.sync.dma_start(raw_tail, x_rows[1, :, 3, T - TAIL :])
+        nc.sync.dma_start(raw_c[:], x_rows[1, :, 0, :])
+        nc.sync.dma_start(raw_d, x_rows[1, :, 1, 0 : T - TAIL])
+        nc.sync.dma_start(raw_tail, x_rows[1, :, 1, T - TAIL :])
 
         s_rows = w_scales.rearrange("e a q n -> q (e a) n")
-        b_rows = b.rearrange("(h p) e -> p h e", p=P)
+        b_rows = b.rearrange("(h p) (i e) -> p h i e", p=P, e=2)
         w_rows = w_words.rearrange("e a p n -> p (e a) n")
 
         def load_scales(ws, x0, x1):
@@ -93,23 +107,20 @@ def tile_moe_two_lin_relu_kernel(tc, xT, w_words, w_scales, b, gate, offs, dst, 
                     ws[32 * q : 32 * q + 4, :, :].bitcast(I32), s_rows[4 * q : 4 * q + 4, x0:x1, :].bitcast(I32)
                 )
 
-        def load_words(ww, i0, i1):
-            nc.sync.dma_start(ww[:].bitcast(I32), w_rows[:, 2 * PASSES * i0 : 2 * PASSES * i1, :].bitcast(I32))
+        def load_words(g):
+            i0, i1 = WEIGHTS[g]
+            nc.sync.dma_start(ww[g][:].bitcast(I32), w_rows[:, 2 * PASSES * i0 : 2 * PASSES * i1, :].bitcast(I32))
 
-        def load_bias(i):
-            nc.sync.dma_start(pairs1[i + AHEAD][:, :, 0:2].bitcast(F32), b_rows[:, :, 2 * i : 2 * i + 2])
-
-        load_words(ww[0], 0, 1)
+        load_words(0)
         load_scales(ws_first, 0, 2 * PASSES)
-        load_bias(0)
+        nc.sync.dma_start(quads1_rest[:, :, 0:2], b_rows[:, 0, :, :])
         nc.sync.dma_start(dst_t[:], dst)
         nc.sync.dma_start(gate_t[:, 0:PIECE], gate[0:P, 0:PIECE])
-        load_words(ww[1], 1, 2)
+        nc.sync.dma_start(unit(0, PIECES).rearrange("p (i s) -> p i s", i=PIECES)[:, :, 0:2], b_rows[:, 1, :, :])
+        load_words(1)
         load_scales(ws_rest, 2 * PASSES, E * PASSES)
-        load_bias(1)
         nc.sync.dma_start(gate_t[:, PIECE:], gate[0:P, PIECE:])
-        load_words(ww[2], 2, PIECES)
-        nc.sync.dma_start(bias[:], b_rows[:, :, 2 * (PIECES - AHEAD) :])
+        load_words(2)
 
         def scalar_cast(o, i):
             nc.scalar.activation(o, i, COPY)
@@ -124,92 +135,99 @@ def tile_moe_two_lin_relu_kernel(tc, xT, w_words, w_scales, b, gate, offs, dst, 
                 raw_pair[u, c][:, :, t0:t1].rearrange("p e t -> p t e"),
             )
 
-        for u in range(2):
+        def round_pair(u):
             for c in range(2):
                 n, v = LOADS[u][c]
                 if v > 0:
                     interleave(nc.vector.tensor_copy, u, c, 0, v)
                 interleave(scalar_cast, u, c, v, n)
+
+        def gather_words(into, u, s0, s1):
             window = win_pair[u][:].rearrange("p t e -> p (t e)").bitcast(U32)
-            for s0, s1 in FIRST:
-                nc.vector.tensor_copy(pairs0[s0][:, u, :], window.indirect(slots(offs_t, s0, s1)))
+            nc.vector.tensor_copy(into, window.indirect(slots(offs_t, s0, s1)))
 
-        scalar_cast(win_row[0][:], raw_row[0])
-        for j in (1, 2):
-            nc.vector.tensor_copy(win_row[j][:], raw_row[j])
-        nc.vector.tensor_copy(win_row[3][:, 0 : T - TAIL], raw_row[3])
-        nc.vector.tensor_copy(win_row[3][:, T - TAIL :], raw_tail)
+        def gather_row(e, i):
+            into = pairs1[i][:, 0, :].bitcast(BF16).rearrange("p (s e) -> p s e", e=2)[:, :, e]
+            nc.scalar.activation(into, win_row[e][:].indirect(slots(offs_t, i * PIECE, (i + 1) * PIECE)), COPY)
 
-        def gather_pair(u, i):
-            for e in range(2):
-                into = pairs1[i][:, u, :].bitcast(BF16).rearrange("p (s e) -> p s e", e=2)[:, :, e]
-                nc.scalar.activation(into, win_row[2 * u + e][:].indirect(slots(offs_t, i * PIECE, (i + 1) * PIECE)), COPY)
+        def gather_third(i):
+            gather_words(pairs1[i][:, 1, :], 2, i * PIECE, (i + 1) * PIECE)
 
         def merge(copy, word, quads, pairs):
-            copy(
-                quads.bitcast(word).rearrange("p (s u) -> p s u", u=2),
-                pairs.bitcast(word).rearrange("p u s -> p s u"),
-            )
+            copy(quads.bitcast(word).rearrange("p (s u) -> p s u", u=2), pairs.bitcast(word).rearrange("p u s -> p s u"))
+
+        def merge1(i):
+            merge(nc.scalar.copy, U32, quads1[i], pairs1[i])
 
         def quantise(codes, planes, quads):
-            nc.vector.quantize_mx(out=codes[:].bitcast(FP8X4), scales=planes[:], in_=quads)
-
-        def finish(i):
-            quads = keep.tile([P, PIECE * PACK], BF16, name=f"quads1_{i}", align_bytes=64)
-            copy, word = (nc.vector.tensor_copy, I32) if i < PIECES - 1 else (nc.scalar.copy, U32)
-            merge(copy, word, quads[:], pairs1[i])
-            quantise(codes1[i], planes1[i], quads[:])
+            nc.vector.quantize_mx(out=codes.bitcast(FP8X4), scales=planes, in_=quads.bitcast(BF16))
 
         for u in range(2):
-            for i in range(AHEAD):
-                gather_pair(u, i)
-        quads_a = raw_row[0][:, 0 : 2 * PIECE].bitcast(BF16)
-        codes0[0] = keep.tile([P, PIECE], U32, name="rawrow2", align_bytes=64)
-        quads_b = last[:, 6 * PIECE : 8 * PIECE].bitcast(BF16)
-        quads_c = last[:, PIECE : 5 * PIECE].bitcast(BF16)
-        merge(nc.vector.tensor_copy, I32, quads_a, pairs0[0][:])
-        quantise(codes0[0], planes0[0], quads_a)
-        merge(nc.vector.tensor_copy, I32, quads_b, pairs0[PIECE][:])
-        merge(nc.vector.tensor_copy, I32, quads_c, pairs0[2 * PIECE][:])
-        finish(0)
-        quantise(codes0[PIECE], planes0[PIECE], quads_b)
-        quantise(codes0[2 * PIECE], planes0[2 * PIECE], quads_c)
-        finish(1)
+            round_pair(u)
+            for s0 in range(0, SLOTS, WIDE):
+                gather_words(pairs0[:, u, s0 : s0 + WIDE], u, s0, s0 + WIDE)
+        round_pair(2)
+        for i in range(2):
+            gather_third(i)
+        for s0 in range(0, SLOTS, WIDE):
+            merge(nc.scalar.copy, U32, quads0[:, 2 * s0 : 2 * (s0 + WIDE)], pairs0[:, :, s0 : s0 + WIDE])
+        nc.vector.tensor_copy(win_row[0][:], raw_c[:])
+        nc.vector.tensor_copy(win_row[1][:, 0 : T - TAIL], raw_d)
+        nc.vector.tensor_copy(win_row[1][:, T - TAIL :], raw_tail)
+        for i in range(2):
+            for e in range(2):
+                gather_row(e, i)
+        codes0 = [keep.tile([P, WIDE], U32, name="raw_d", align_bytes=64)]
+        quantise(codes0[0][:], planes0[0][:], quads0[:, 0 : 2 * WIDE])
+        gather_third(2)
+        for e in range(2):
+            merge(nc.vector.tensor_copy, I32, quads1[0][:, e * PIECE : (e + 1) * PIECE], pairs1[0][:, :, e * C : (e + 1) * C])
+        for e in range(2):
+            cols = slice(e * C, (e + 1) * C)
+            quantise(codes1[0][:, cols], planes1[0][:, cols], quads1[0][:, e * PIECE : (e + 1) * PIECE])
+        codes0.append(keep.tile([P, WIDE], U32, name="pairs1_first", align_bytes=64))
+        quantise(codes0[1][:], planes0[1][:], quads0[:, 2 * WIDE :])
+        gather_third(3)
 
         for i in range(PIECES):
             acc = {}
-            g0 = max(s0 for s0, s1 in FIRST if s0 <= i * PIECE)
+            g = max(g for g in range(len(WEIGHTS)) if WEIGHTS[g][0] <= i)
             for a in range(PASSES):
                 for h in range(HALVES):
                     for e in range(2):
                         if a == 0:
                             acc[h, e] = psum.tile([P, C], F32, name=f"acc{h}_{e}")
                         ws = ws_first[:, e * PASSES + a, :] if i == 0 else ws_rest[:, (2 * i + e - 2) * PASSES + a, :]
-                        c0 = e * C + (i * PIECE - g0 if a == 0 else 0)
+                        c0 = e * C + (i % 2 * PIECE if a == 0 else 0)
+                        x = (2 * (i - WEIGHTS[g][0]) + e) * PASSES + a
                         nc.tensor.matmul_mx(
                             out=acc[h, e][:],
-                            lhsT=ww[g0 // PIECE][:, (2 * i + e - g0 // C) * PASSES + a, h * 2 * P : (h + 1) * 2 * P].bitcast(FP4X4),
+                            lhsT=ww[g][:, x, h * 2 * P : (h + 1) * 2 * P].bitcast(FP4X4),
                             lhsT_scale=ws[:, h * P : (h + 1) * P],
-                            rhs=(codes0[g0], codes1[i])[a][:, c0 : c0 + C].bitcast(FP8X4),
-                            rhs_scale=(planes0[g0], planes1[i])[a][:, c0 : c0 + C],
+                            rhs=(codes0[i // 2], codes1[i])[a][:, c0 : c0 + C].bitcast(FP8X4),
+                            rhs_scale=(planes0[i // 2], planes1[i])[a][:, c0 : c0 + C],
                             start=(a == 0),
                             stop=(a == PASSES - 1),
                         )
             for h in range(HALVES):
-                y = keep.tile([P, PIECE], F32, name=f"y{h}_{i}")
+                if h == 1 and i + 1 < PIECES:
+                    merge1(i + 1)
+                    quantise(codes1[i + 1][:], planes1[i + 1][:], quads1[i + 1])
+                    y = unit(PLACES[i][0])
+                else:
+                    y = keep.tile([P, PIECE], F32, name=f"y{h}_{i}")[:]
                 for e in range(2):
                     nc.scalar.activation(
                         y[:, e * C : (e + 1) * C], acc[h, e][:], RELU, bias=bias_of(h, i)[:, e : e + 1]
                     )
                 nc.vector.tensor_tensor(
                     out_t[h][:].indirect(slots(dst_t, i * PIECE, (i + 1) * PIECE)),
-                    y[:],
+                    y,
                     gate_t[:, i * PIECE : (i + 1) * PIECE],
                     MULT,
                 )
-                if i + AHEAD < PIECES:
-                    gather_pair(h, i + AHEAD)
-            if i + AHEAD < PIECES:
-                finish(i + AHEAD)
+            if i + 2 < PIECES:
+                for e in range(2):
+                    gather_row(e, i + 2)
         for h in range(HALVES):
             nc.sync.dma_start(out[h * P : (h + 1) * P, :], out_t[h][:])

@@ -13,7 +13,7 @@ PIECE = 2 * C
 PIECES = SLOTS // PIECE
 WIDE = 2 * PIECE
 TAIL = 384
-PLACES = ((5, 6), (0, 4), (1, 7))
+PLACES = ((5, 6), (0, 9), (1, 4))
 WEIGHTS = ((0, 1), (1, 2), (2, PIECES))
 
 F32 = mybir.dt.float32
@@ -28,7 +28,7 @@ COPY = mybir.ActivationFunctionType.Copy
 RELU = mybir.ActivationFunctionType.Relu
 MULT = mybir.AluOpType.mult
 
-LOADS = (((896, 576), (384, 256)), ((640, 0), (640, 416)), ((640, 0), (640, 352)))
+LOADS = (((896, 576), (384, 208)), ((640, 0), (640, 320)), ((640, 0), (640, 256)))
 PAIRS = ((0, 0), (0, 2), (1, 2))
 
 
@@ -40,14 +40,14 @@ def tile_moe_two_lin_relu_kernel(tc, xT, w_words, w_scales, b, gate, offs, dst, 
 
         offs_t = keep.tile([P, SLOTS // 16], U16, name="offs_t")
         dst_t = keep.tile([P, SLOTS // 16], U16, name="dst_t")
-        ww = [keep.tile([P, 2 * (i1 - i0) * PASSES, 2 * N], U8, name=f"ww{i0}", align_bytes=64) for i0, i1 in WEIGHTS]
+        ww = [keep.tile([P, 2 * (i1 - i0) * PASSES, 2 * N], U8, name=f"ww{i0}", align_bytes=256) for i0, i1 in WEIGHTS]
         ws_first = keep.tile([P, 2 * PASSES, N], U8, name="ws_first", align_bytes=64)
         ws_rest = keep.tile([P, (E - 2) * PASSES, N], U8, name="ws_rest", align_bytes=64)
-        gate_t = keep.tile([P, SLOTS], F32, name="gate_t")
-        out_t = [keep.tile([P, T], F32, name=f"out{h}") for h in range(HALVES)]
+        gate_t = keep.tile([P, SLOTS], F32, name="gate_t", align_bytes=256)
+        out_t = [keep.tile([P, T], F32, name=f"out{h}", align_bytes=256) for h in range(HALVES)]
 
-        quads0 = keep.tile([P, 2 * SLOTS], F32, name="quads0", align_bytes=64)
-        shared = keep.tile([P, 13 * PIECE], F32, name="shared", align_bytes=64)
+        quads0 = keep.tile([P, 2 * SLOTS], F32, name="quads0", align_bytes=256)
+        shared = keep.tile([P, 18 * PIECE], F32, name="shared", align_bytes=256)
 
         def unit(n, count=1):
             return shared[:, n * PIECE : (n + count) * PIECE]
@@ -61,14 +61,14 @@ def tile_moe_two_lin_relu_kernel(tc, xT, w_words, w_scales, b, gate, offs, dst, 
             pairs1.append(both.bitcast(U32).rearrange("p (u s) -> p u s", u=2)[:, :, 0:PIECE])
 
         raw_pair = {
-            (u, c): keep.tile([P, 2, LOADS[u][c][0]], F32, name=f"rawpair{u}_{c}")[:]
+            (u, c): keep.tile([P, 2, LOADS[u][c][0]], F32, name=f"rawpair{u}_{c}", align_bytes=256)[:]
             for u in range(3)
             for c in range(2)
             if (u, c) != (2, 1)
         }
         raw_pair[2, 1] = quads0[:, 0 : 2 * LOADS[2][1][0]].rearrange("p (e t) -> p e t", e=2)
-        raw_c = keep.tile([P, T], F32, name="raw_c")
-        raw_d = keep.tile([P, T - TAIL], F32, name="raw_d", align_bytes=64)[:]
+        raw_c = keep.tile([P, T], F32, name="raw_c", align_bytes=256)
+        raw_d = keep.tile([P, T - TAIL], F32, name="raw_d", align_bytes=256)[:]
         raw_tail = shared[:, 5 * PIECE - TAIL // 2 : 5 * PIECE + TAIL // 2]
         win_pair = [keep.tile([P, T, 2], BF16, name=f"winpair{u}") for u in range(3)]
         win_row = [keep.tile([P, T], BF16, name=f"winrow{j}") for j in range(2)]
@@ -171,15 +171,16 @@ def tile_moe_two_lin_relu_kernel(tc, xT, w_words, w_scales, b, gate, offs, dst, 
             gather_third(i)
         for s0 in range(0, SLOTS, WIDE):
             merge(nc.scalar.copy, U32, quads0[:, 2 * s0 : 2 * (s0 + WIDE)], pairs0[:, :, s0 : s0 + WIDE])
-        nc.vector.tensor_copy(win_row[0][:], raw_c[:])
+        gather_third(2)
+        nc.gpsimd.tensor_copy(win_row[0][:], raw_c[:])
         nc.vector.tensor_copy(win_row[1][:, 0 : T - TAIL], raw_d)
         nc.vector.tensor_copy(win_row[1][:, T - TAIL :], raw_tail)
         for i in range(2):
             for e in range(2):
                 gather_row(e, i)
-        codes0 = [keep.tile([P, WIDE], U32, name="raw_d", align_bytes=64)]
+        codes0 = [keep.tile([P, WIDE], U32, name="raw_d", align_bytes=256)]
         quantise(codes0[0][:], planes0[0][:], quads0[:, 0 : 2 * WIDE])
-        gather_third(2)
+        gather_third(3)
         for e in range(2):
             merge(nc.vector.tensor_copy, I32, quads1[0][:, e * PIECE : (e + 1) * PIECE], pairs1[0][:, :, e * C : (e + 1) * C])
         for e in range(2):
@@ -187,7 +188,6 @@ def tile_moe_two_lin_relu_kernel(tc, xT, w_words, w_scales, b, gate, offs, dst, 
             quantise(codes1[0][:, cols], planes1[0][:, cols], quads1[0][:, e * PIECE : (e + 1) * PIECE])
         codes0.append(keep.tile([P, WIDE], U32, name="pairs1_first", align_bytes=64))
         quantise(codes0[1][:], planes0[1][:], quads0[:, 2 * WIDE :])
-        gather_third(3)
 
         for i in range(PIECES):
             acc = {}

@@ -12,8 +12,8 @@ HALVES = N // P
 PIECE = 2 * C
 PIECES = SLOTS // PIECE
 WIDE = 2 * PIECE
-TAIL = 384
-PLACES = ((5, 6), (0, 9), (1, 4))
+TAIL = 640
+PLACES = ((6, 11), (7, 12), (0, 4), (1, 5))
 WEIGHTS = ((0, 1), (1, 2), (2, PIECES))
 
 F32 = mybir.dt.float32
@@ -28,7 +28,7 @@ COPY = mybir.ActivationFunctionType.Copy
 RELU = mybir.ActivationFunctionType.Relu
 MULT = mybir.AluOpType.mult
 
-LOADS = (((896, 576), (384, 208)), ((640, 0), (640, 320)), ((640, 0), (640, 256)))
+LOADS = (((896, 576), (384, 208)), ((640, 0), (640, 320)), ((640, 0), (640, 352)))
 PAIRS = ((0, 0), (0, 2), (1, 2))
 
 
@@ -46,16 +46,19 @@ def tile_moe_two_lin_relu_kernel(tc, xT, w_words, w_scales, b, gate, offs, dst, 
         gate_t = keep.tile([P, SLOTS], F32, name="gate_t", align_bytes=256)
         out_t = [keep.tile([P, T], F32, name=f"out{h}", align_bytes=256) for h in range(HALVES)]
 
-        quads0 = keep.tile([P, 2 * SLOTS], F32, name="quads0", align_bytes=256)
-        shared = keep.tile([P, 18 * PIECE], F32, name="shared", align_bytes=256)
+        shared = keep.tile([P, 17 * PIECE], F32, name="shared", align_bytes=256)
 
         def unit(n, count=1):
             return shared[:, n * PIECE : (n + count) * PIECE]
 
-        quads1_rest = keep.tile([P, PIECES, 2 * PIECE], F32, name="quads1_rest", align_bytes=64)
-        quads1 = [unit(7, 2)] + [quads1_rest[:, i, :] for i in range(PIECES - 1)]
+        quads0_early = keep.tile([P, 2, WIDE], F32, name="quads0_early", align_bytes=64)
+        quads0_late = keep.tile([P, WIDE + TAIL], F32, name="quads0_late", align_bytes=256)
+        quads0 = [quads0_early[:, 0, :], quads0_early[:, 1, :], quads0_late[:, 0:WIDE], quads0_late[:, WIDE : 2 * WIDE]]
+        quads1_rest = keep.tile([P, PIECES, WIDE], F32, name="quads1_rest", align_bytes=64)
+        quads1 = [keep.tile([P, WIDE], F32, name=f"quads1_{i}", align_bytes=64)[:] for i in range(2)]
+        quads1 = quads1 + [quads1_rest[:, i, :] for i in range(1, PIECES - 1)]
         pairs0 = keep.tile([P, 2, SLOTS], U32, name="pairs0")
-        pairs1 = [keep.tile([P, 2, PIECE], U32, name="pairs1_first", align_bytes=64)[:]]
+        pairs1 = []
         for rows, words in PLACES:
             both = unit(rows, 2 * (words - rows))
             pairs1.append(both.bitcast(U32).rearrange("p (u s) -> p u s", u=2)[:, :, 0:PIECE])
@@ -66,13 +69,18 @@ def tile_moe_two_lin_relu_kernel(tc, xT, w_words, w_scales, b, gate, offs, dst, 
             for c in range(2)
             if (u, c) != (2, 1)
         }
-        raw_pair[2, 1] = quads0[:, 0 : 2 * LOADS[2][1][0]].rearrange("p (e t) -> p e t", e=2)
+        raw_pair[2, 1] = unit(6, 5).rearrange("p (e t) -> p e t", e=2)
         raw_c = keep.tile([P, T], F32, name="raw_c", align_bytes=256)
         raw_d = keep.tile([P, T - TAIL], F32, name="raw_d", align_bytes=256)[:]
-        raw_tail = shared[:, 5 * PIECE - TAIL // 2 : 5 * PIECE + TAIL // 2]
+        raw_tail = quads0_late[:, WIDE:]
         win_pair = [keep.tile([P, T, 2], BF16, name=f"winpair{u}") for u in range(3)]
         win_row = [keep.tile([P, T], BF16, name=f"winrow{j}") for j in range(2)]
-        planes0 = [keep.tile([P, WIDE], U8, name=f"planes0_{g}", align_bytes=64) for g in range(2)]
+        planes0_early = keep.tile([P, WIDE], U8, name="planes0_early", align_bytes=64)
+        codes0_early = keep.tile([P, WIDE], U32, name="codes0_early", align_bytes=64)
+        planes0 = [planes0_early[:, 0:PIECE], planes0_early[:, PIECE:]]
+        planes0_late = keep.tile([P, WIDE], U8, name="planes0_late", align_bytes=64)
+        planes0 = planes0 + [planes0_late[:, 0:PIECE], planes0_late[:, PIECE:]]
+        codes0 = [codes0_early[:, 0:PIECE], codes0_early[:, PIECE:]]
         codes1 = [keep.tile([P, PIECE], U32, name=f"codes1_{i}", align_bytes=64) for i in range(PIECES)]
         planes1 = [keep.tile([P, PIECE], U8, name=f"planes1_{i}", align_bytes=64) for i in range(PIECES)]
 
@@ -93,7 +101,8 @@ def tile_moe_two_lin_relu_kernel(tc, xT, w_words, w_scales, b, gate, offs, dst, 
                 nc.sync.dma_start(raw_pair[u, c], x_rows[a, :, j : j + 2, t0 : t0 + LOADS[u][c][0]])
             if u == 0:
                 nc.sync.dma_start(offs_t[:], offs)
-        nc.sync.dma_start(raw_c[:], x_rows[1, :, 0, :])
+            if u == 1:
+                nc.sync.dma_start(raw_c[:], x_rows[1, :, 0, :])
         nc.sync.dma_start(raw_d, x_rows[1, :, 1, 0 : T - TAIL])
         nc.sync.dma_start(raw_tail, x_rows[1, :, 1, T - TAIL :])
 
@@ -162,32 +171,38 @@ def tile_moe_two_lin_relu_kernel(tc, xT, w_words, w_scales, b, gate, offs, dst, 
         def quantise(codes, planes, quads):
             nc.vector.quantize_mx(out=codes.bitcast(FP8X4), scales=planes, in_=quads.bitcast(BF16))
 
+        def merge0(copy, word, i):
+            merge(copy, word, quads0[i], pairs0[:, :, i * PIECE : (i + 1) * PIECE])
+
         for u in range(2):
             round_pair(u)
-            for s0 in range(0, SLOTS, WIDE):
-                gather_words(pairs0[:, u, s0 : s0 + WIDE], u, s0, s0 + WIDE)
-        round_pair(2)
-        for i in range(2):
-            gather_third(i)
-        for s0 in range(0, SLOTS, WIDE):
-            merge(nc.scalar.copy, U32, quads0[:, 2 * s0 : 2 * (s0 + WIDE)], pairs0[:, :, s0 : s0 + WIDE])
-        gather_third(2)
+            step = (WIDE, PIECE)[u]
+            for s0 in range(0, SLOTS, step):
+                gather_words(pairs0[:, u, s0 : s0 + step], u, s0, s0 + step)
         nc.gpsimd.tensor_copy(win_row[0][:], raw_c[:])
-        nc.vector.tensor_copy(win_row[1][:, 0 : T - TAIL], raw_d)
-        nc.vector.tensor_copy(win_row[1][:, T - TAIL :], raw_tail)
         for i in range(2):
-            for e in range(2):
+            merge0(nc.scalar.copy, U32, i)
+        merge0(nc.vector.tensor_copy, I32, 2)
+        quantise(codes0_early[:], planes0_early[:], quads0_early[:].rearrange("p i s -> p (i s)"))
+        round_pair(2)
+        for i in range(PIECES):
+            gather_third(i)
+        nc.gpsimd.tensor_copy(win_row[1][:, 0 : T - TAIL], raw_d)
+        nc.gpsimd.tensor_copy(win_row[1][:, T - TAIL :], raw_tail)
+        merge0(nc.gpsimd.tensor_copy, I32, 3)
+        for e in range(2):
+            for i in range(2):
                 gather_row(e, i)
-        codes0 = [keep.tile([P, WIDE], U32, name="raw_d", align_bytes=256)]
-        quantise(codes0[0][:], planes0[0][:], quads0[:, 0 : 2 * WIDE])
-        gather_third(3)
         for e in range(2):
             merge(nc.vector.tensor_copy, I32, quads1[0][:, e * PIECE : (e + 1) * PIECE], pairs1[0][:, :, e * C : (e + 1) * C])
         for e in range(2):
             cols = slice(e * C, (e + 1) * C)
             quantise(codes1[0][:, cols], planes1[0][:, cols], quads1[0][:, e * PIECE : (e + 1) * PIECE])
-        codes0.append(keep.tile([P, WIDE], U32, name="pairs1_first", align_bytes=64))
-        quantise(codes0[1][:], planes0[1][:], quads0[:, 2 * WIDE :])
+        codes0_late = keep.tile([P, WIDE], U32, name="quads1_0", align_bytes=64)
+        codes0 = codes0 + [codes0_late[:, 0:PIECE], codes0_late[:, PIECE:]]
+        quantise(codes0_late[:], planes0_late[:], quads0_late[:, 0 : 2 * WIDE])
+        merge1(1)
+        quantise(codes1[1][:], planes1[1][:], quads1[1])
 
         for i in range(PIECES):
             acc = {}
@@ -198,22 +213,22 @@ def tile_moe_two_lin_relu_kernel(tc, xT, w_words, w_scales, b, gate, offs, dst, 
                         if a == 0:
                             acc[h, e] = psum.tile([P, C], F32, name=f"acc{h}_{e}")
                         ws = ws_first[:, e * PASSES + a, :] if i == 0 else ws_rest[:, (2 * i + e - 2) * PASSES + a, :]
-                        c0 = e * C + (i % 2 * PIECE if a == 0 else 0)
+                        c0 = e * C
                         x = (2 * (i - WEIGHTS[g][0]) + e) * PASSES + a
                         nc.tensor.matmul_mx(
                             out=acc[h, e][:],
                             lhsT=ww[g][:, x, h * 2 * P : (h + 1) * 2 * P].bitcast(FP4X4),
                             lhsT_scale=ws[:, h * P : (h + 1) * P],
-                            rhs=(codes0[i // 2], codes1[i])[a][:, c0 : c0 + C].bitcast(FP8X4),
-                            rhs_scale=(planes0[i // 2], planes1[i])[a][:, c0 : c0 + C],
+                            rhs=(codes0[i], codes1[i])[a][:, c0 : c0 + C].bitcast(FP8X4),
+                            rhs_scale=(planes0[i], planes1[i])[a][:, c0 : c0 + C],
                             start=(a == 0),
                             stop=(a == PASSES - 1),
                         )
             for h in range(HALVES):
-                if h == 1 and i + 1 < PIECES:
+                if h == 1 and 0 < i < PIECES - 1:
                     merge1(i + 1)
                     quantise(codes1[i + 1][:], planes1[i + 1][:], quads1[i + 1])
-                    y = unit(PLACES[i][0])
+                    y = unit(PLACES[i + 1][0])
                 else:
                     y = keep.tile([P, PIECE], F32, name=f"y{h}_{i}")[:]
                 for e in range(2):

@@ -10,11 +10,8 @@ PACK = 4
 PASSES = K // (P * PACK)
 HALVES = N // P
 PIECE = 2 * C
-PIECES = SLOTS // PIECE
 WIDE = 2 * PIECE
-TAIL = 640
-PLACES = ((6, 11), (7, 12), (0, 4), (1, 5))
-WEIGHTS = ((0, 1), (1, 2), (2, PIECES))
+STAGE = E // 2
 
 F32 = mybir.dt.float32
 BF16 = mybir.dt.bfloat16
@@ -28,8 +25,10 @@ COPY = mybir.ActivationFunctionType.Copy
 RELU = mybir.ActivationFunctionType.Relu
 MULT = mybir.AluOpType.mult
 
-LOADS = (((896, 576), (384, 208)), ((640, 0), (640, 320)), ((640, 0), (640, 352)))
-PAIRS = ((0, 0), (0, 2), (1, 2))
+LOADS = (((896, 576), (384, 208)), ((640, 0), (640, 320)), ((640, 0), (640, 320)), ((640, 0), (640, 320)))
+SCALAR_CUTS = (0, 384, 768, 1024)
+VECTOR_CUTS = (0, 288, 672, 1024)
+WEIGHTS = ((0, 2), (2, 4), (4, 8))
 
 
 def tile_moe_two_lin_relu_kernel(tc, xT, w_words, w_scales, b, gate, offs, dst, out):
@@ -40,96 +39,84 @@ def tile_moe_two_lin_relu_kernel(tc, xT, w_words, w_scales, b, gate, offs, dst, 
 
         offs_t = keep.tile([P, SLOTS // 16], U16, name="offs_t")
         dst_t = keep.tile([P, SLOTS // 16], U16, name="dst_t")
-        ww = [keep.tile([P, 2 * (i1 - i0) * PASSES, 2 * N], U8, name=f"ww{i0}", align_bytes=256) for i0, i1 in WEIGHTS]
-        ws_first = keep.tile([P, 2 * PASSES, N], U8, name="ws_first", align_bytes=64)
-        ws_rest = keep.tile([P, (E - 2) * PASSES, N], U8, name="ws_rest", align_bytes=64)
-        gate_t = keep.tile([P, SLOTS], F32, name="gate_t", align_bytes=256)
-        out_t = [keep.tile([P, T], F32, name=f"out{h}", align_bytes=256) for h in range(HALVES)]
+        ww = [keep.tile([P, (e1 - e0) * PASSES, 2 * N], U8, name=f"ww{e0}", align_bytes=256) for e0, e1 in WEIGHTS]
+        ws = [keep.tile([P, STAGE * PASSES, N], U8, name=f"ws{s}", align_bytes=64) for s in range(2)]
+        gate_all = keep.tile([P, SLOTS], F32, name="gate_all", align_bytes=256)
+        bias_t = keep.tile([P, HALVES, E], F32, name="bias_t")
+        window0 = keep.tile([P, T + 2 * WIDE], F32, name="window0", align_bytes=256)
+        window1 = keep.tile([P, T], F32, name="window1", align_bytes=256)
+        windows = (window0, window1)
+        late = keep.tile([P, 2 * SLOTS - SCALAR_CUTS[1]], F32, name="late", align_bytes=64)
+        y = [keep.tile([P, SLOTS], F32, name="y0", align_bytes=64)[:], late[:, SLOTS - SCALAR_CUTS[1] :]]
+        gated = keep.tile([P, SLOTS], F32, name="gated", align_bytes=64)
 
-        shared = keep.tile([P, 17 * PIECE], F32, name="shared", align_bytes=256)
-
-        def unit(n, count=1):
-            return shared[:, n * PIECE : (n + count) * PIECE]
-
-        quads0_early = keep.tile([P, 2, WIDE], F32, name="quads0_early", align_bytes=64)
-        quads0_late = keep.tile([P, WIDE + TAIL], F32, name="quads0_late", align_bytes=256)
-        quads0 = [quads0_early[:, 0, :], quads0_early[:, 1, :], quads0_late[:, 0:WIDE], quads0_late[:, WIDE : 2 * WIDE]]
-        quads1_rest = keep.tile([P, PIECES, WIDE], F32, name="quads1_rest", align_bytes=64)
-        quads1 = [keep.tile([P, WIDE], F32, name=f"quads1_{i}", align_bytes=64)[:] for i in range(2)]
-        quads1 = quads1 + [quads1_rest[:, i, :] for i in range(1, PIECES - 1)]
-        pairs0 = keep.tile([P, 2, SLOTS], U32, name="pairs0")
-        pairs1 = []
-        for rows, words in PLACES:
-            both = unit(rows, 2 * (words - rows))
-            pairs1.append(both.bitcast(U32).rearrange("p (u s) -> p u s", u=2)[:, :, 0:PIECE])
-
-        raw_pair = {
-            (u, c): keep.tile([P, 2, LOADS[u][c][0]], F32, name=f"rawpair{u}_{c}", align_bytes=256)[:]
-            for u in range(3)
+        last_loads = keep.tile([P, 2 * T + 2 * WIDE], F32, name="last_loads", align_bytes=256)
+        raw = {
+            (u, c): keep.tile([P, 2 * LOADS[u][c][0]], F32, name=f"raw{u}_{c}", align_bytes=256)[:]
+            for u in range(4)
             for c in range(2)
-            if (u, c) != (2, 1)
+            if u < 2 or c == 0
         }
-        raw_pair[2, 1] = unit(6, 5).rearrange("p (e t) -> p e t", e=2)
-        raw_c = keep.tile([P, T], F32, name="raw_c", align_bytes=256)
-        raw_d = keep.tile([P, T - TAIL], F32, name="raw_d", align_bytes=256)[:]
-        raw_tail = quads0_late[:, WIDE:]
-        win_pair = [keep.tile([P, T, 2], BF16, name=f"winpair{u}") for u in range(3)]
-        win_row = [keep.tile([P, T], BF16, name=f"winrow{j}") for j in range(2)]
-        planes0_early = keep.tile([P, WIDE], U8, name="planes0_early", align_bytes=64)
-        codes0_early = keep.tile([P, WIDE], U32, name="codes0_early", align_bytes=64)
-        planes0 = [planes0_early[:, 0:PIECE], planes0_early[:, PIECE:]]
-        planes0_late = keep.tile([P, WIDE], U8, name="planes0_late", align_bytes=64)
-        planes0 = planes0 + [planes0_late[:, 0:PIECE], planes0_late[:, PIECE:]]
-        codes0 = [codes0_early[:, 0:PIECE], codes0_early[:, PIECE:]]
-        codes1 = [keep.tile([P, PIECE], U32, name=f"codes1_{i}", align_bytes=64) for i in range(PIECES)]
-        planes1 = [keep.tile([P, PIECE], U8, name=f"planes1_{i}", align_bytes=64) for i in range(PIECES)]
+        raw[2, 1] = last_loads[:, 0:T]
+        raw[3, 1] = last_loads[:, T : 2 * T]
+        win = [keep.tile([P, T, 2], BF16, name=f"win{u}") for u in range(4)]
+        pairs = {(0, s): keep.tile([P, 2 * WIDE], U32, name=f"pairs0_{s}", align_bytes=64)[:] for s in range(2)}
+        pairs[1, 0] = last_loads[:, 2 * T :].bitcast(U32)
+        pairs[1, 1] = window0[:, T:].bitcast(U32)
+        early = last_loads[:, T - WIDE : T + WIDE].bitcast(U32)
+        across = last_loads[:, 2 * T - WIDE : 2 * T + WIDE].bitcast(U32)
+        quads = {
+            (0, 0): early,
+            (0, 1): early[:, WIDE:],
+            (0, 2): across,
+            (0, 3): across[:, WIDE:],
+            (1, 0): pairs[1, 1][:, WIDE:],
+            (1, 1): keep.tile([P, WIDE], U32, name="quads1_1", align_bytes=64)[:],
+            (1, 2): late[:, 0:WIDE].bitcast(U32),
+            (1, 3): late[:, WIDE:SLOTS].bitcast(U32),
+        }
+        codes = {(a, s): keep.tile([P, WIDE], U32, name=f"codes{a}_{s}", align_bytes=64) for a in range(PASSES) for s in range(2)}
+        planes = {(a, s): keep.tile([P, WIDE], U8, name=f"planes{a}_{s}", align_bytes=64) for a in range(PASSES) for s in range(2)}
 
-        nc.vector.memset(ws_first[:].rearrange("p x n -> p (x n)").bitcast(I32), 0)
-        nc.vector.memset(ws_rest[:].rearrange("p x n -> p (x n)").bitcast(I32), 0)
+        for s in range(2):
+            nc.vector.memset(ws[s][:].rearrange("p x n -> p (x n)").bitcast(I32), 0)
         for h in range(HALVES):
-            nc.gpsimd.memset(out_t[h][:], 0.0)
+            nc.gpsimd.memset(windows[h][:, 0:T], 0.0)
 
-        def bias_of(h, i):
-            if h == 0:
-                return quads1_rest[:, i, 0:2]
-            return unit(i)[:, 0:2]
-
-        x_rows = xT.rearrange("(a p j) t -> a p j t", p=P, j=PACK)
-        for u, (a, j) in enumerate(PAIRS):
+        x_rows = xT.rearrange("(u p j) t -> u p j t", p=P, j=PACK)
+        for u in range(4):
+            a, j = u // 2, 2 * (u % 2)
             for c in range(2):
                 t0 = c * LOADS[u][0][0]
-                nc.sync.dma_start(raw_pair[u, c], x_rows[a, :, j : j + 2, t0 : t0 + LOADS[u][c][0]])
+                nc.sync.dma_start(
+                    raw[u, c].rearrange("p (e t) -> p e t", e=2), x_rows[a, :, j : j + 2, t0 : t0 + LOADS[u][c][0]]
+                )
             if u == 0:
                 nc.sync.dma_start(offs_t[:], offs)
-            if u == 1:
-                nc.sync.dma_start(raw_c[:], x_rows[1, :, 0, :])
-        nc.sync.dma_start(raw_d, x_rows[1, :, 1, 0 : T - TAIL])
-        nc.sync.dma_start(raw_tail, x_rows[1, :, 1, T - TAIL :])
 
         s_rows = w_scales.rearrange("e a q n -> q (e a) n")
-        b_rows = b.rearrange("(h p) (i e) -> p h i e", p=P, e=2)
         w_rows = w_words.rearrange("e a p n -> p (e a) n")
 
-        def load_scales(ws, x0, x1):
+        def load_scales(s):
             for q in range(4):
                 nc.sync.dma_start(
-                    ws[32 * q : 32 * q + 4, :, :].bitcast(I32), s_rows[4 * q : 4 * q + 4, x0:x1, :].bitcast(I32)
+                    ws[s][32 * q : 32 * q + 4, :, :].bitcast(I32),
+                    s_rows[4 * q : 4 * q + 4, s * STAGE * PASSES : (s + 1) * STAGE * PASSES, :].bitcast(I32),
                 )
 
         def load_words(g):
-            i0, i1 = WEIGHTS[g]
-            nc.sync.dma_start(ww[g][:].bitcast(I32), w_rows[:, 2 * PASSES * i0 : 2 * PASSES * i1, :].bitcast(I32))
+            e0, e1 = WEIGHTS[g]
+            nc.sync.dma_start(ww[g][:].bitcast(I32), w_rows[:, PASSES * e0 : PASSES * e1, :].bitcast(I32))
 
         load_words(0)
-        load_scales(ws_first, 0, 2 * PASSES)
-        nc.sync.dma_start(quads1_rest[:, :, 0:2], b_rows[:, 0, :, :])
-        nc.sync.dma_start(dst_t[:], dst)
-        nc.sync.dma_start(gate_t[:, 0:PIECE], gate[0:P, 0:PIECE])
-        nc.sync.dma_start(unit(0, PIECES).rearrange("p (i s) -> p i s", i=PIECES)[:, :, 0:2], b_rows[:, 1, :, :])
+        load_scales(0)
+        nc.sync.dma_start(bias_t[:], b.rearrange("(h p) e -> p h e", p=P))
         load_words(1)
-        load_scales(ws_rest, 2 * PASSES, E * PASSES)
-        nc.sync.dma_start(gate_t[:, PIECE:], gate[0:P, PIECE:])
+        nc.sync.dma_start(gate_all[:, 0:WIDE], gate[0:P, 0:WIDE])
+        nc.sync.dma_start(dst_t[:], dst)
         load_words(2)
+        load_scales(1)
+        nc.sync.dma_start(gate_all[:, WIDE:], gate[0:P, WIDE:])
 
         def scalar_cast(o, i):
             nc.scalar.activation(o, i, COPY)
@@ -140,8 +127,8 @@ def tile_moe_two_lin_relu_kernel(tc, xT, w_words, w_scales, b, gate, offs, dst, 
         def interleave(copy, u, c, t0, t1):
             first = c * LOADS[u][0][0]
             copy(
-                win_pair[u][:, first + t0 : first + t1, :],
-                raw_pair[u, c][:, :, t0:t1].rearrange("p e t -> p t e"),
+                win[u][:, first + t0 : first + t1, :],
+                raw[u, c].rearrange("p (e t) -> p t e", e=2)[:, t0:t1, :],
             )
 
         def round_pair(u):
@@ -151,98 +138,103 @@ def tile_moe_two_lin_relu_kernel(tc, xT, w_words, w_scales, b, gate, offs, dst, 
                     interleave(nc.vector.tensor_copy, u, c, 0, v)
                 interleave(scalar_cast, u, c, v, n)
 
-        def gather_words(into, u, s0, s1):
-            window = win_pair[u][:].rearrange("p t e -> p (t e)").bitcast(U32)
-            nc.vector.tensor_copy(into, window.indirect(slots(offs_t, s0, s1)))
+        def gather(u, s, s0, s1):
+            window = win[u][:].rearrange("p t e -> p (t e)").bitcast(U32)
+            first = (u % 2) * WIDE
+            nc.vector.tensor_copy(
+                pairs[u // 2, s][:, first + s0 : first + s1], window.indirect(slots(offs_t, s * WIDE + s0, s * WIDE + s1))
+            )
 
-        def gather_row(e, i):
-            into = pairs1[i][:, 0, :].bitcast(BF16).rearrange("p (s e) -> p s e", e=2)[:, :, e]
-            nc.scalar.activation(into, win_row[e][:].indirect(slots(offs_t, i * PIECE, (i + 1) * PIECE)), COPY)
+        def merge(copy, word, a, s, s0, s1):
+            copy(
+                quads[a, 2 * s + s0 // PIECE][:, 0 : 2 * (s1 - s0)].bitcast(word).rearrange("p (s u) -> p s u", u=2),
+                pairs[a, s].bitcast(word).rearrange("p (u s) -> p s u", u=2)[:, s0:s1, :],
+            )
 
-        def gather_third(i):
-            gather_words(pairs1[i][:, 1, :], 2, i * PIECE, (i + 1) * PIECE)
+        def quantise(a, s, s0, s1):
+            nc.vector.quantize_mx(
+                out=codes[a, s][:, s0:s1].bitcast(FP8X4), scales=planes[a, s][:, s0:s1], in_=quads[a, 2 * s + s0 // PIECE][:, 0 : 2 * (s1 - s0)].bitcast(BF16)
+            )
 
-        def merge(copy, word, quads, pairs):
-            copy(quads.bitcast(word).rearrange("p (s u) -> p s u", u=2), pairs.bitcast(word).rearrange("p u s -> p s u"))
+        acc = {}
 
-        def merge1(i):
-            merge(nc.scalar.copy, U32, quads1[i], pairs1[i])
+        def multiply(a, h, e):
+            s, i = divmod(e, STAGE)
+            g = max(g for g in range(len(WEIGHTS)) if WEIGHTS[g][0] <= e)
+            if a == 0 and e % 2 == 0:
+                bank = psum.tile([P, PIECE], F32, name=f"acc{h}_{e // 2}")
+                acc[h, e] = bank[:, 0:C]
+                acc[h, e + 1] = bank[:, C:]
+            nc.tensor.matmul_mx(
+                out=acc[h, e],
+                lhsT=ww[g][:, (e - WEIGHTS[g][0]) * PASSES + a, h * 2 * P : (h + 1) * 2 * P].bitcast(FP4X4),
+                lhsT_scale=ws[s][:, i * PASSES + a, h * P : (h + 1) * P],
+                rhs=codes[a, s][:, i * C : (i + 1) * C].bitcast(FP8X4),
+                rhs_scale=planes[a, s][:, i * C : (i + 1) * C],
+                start=(a == 0 and e % 2 == 0),
+                stop=(a == PASSES - 1 and e % 2 == 1),
+            )
 
-        def quantise(codes, planes, quads):
-            nc.vector.quantize_mx(out=codes.bitcast(FP8X4), scales=planes, in_=quads.bitcast(BF16))
+        def activate(h, e):
+            nc.scalar.activation(y[h][:, e * C : (e + 1) * C], acc[h, e], RELU, bias=bias_t[:, h, e : e + 1])
 
-        def merge0(copy, word, i):
-            merge(copy, word, quads0[i], pairs0[:, :, i * PIECE : (i + 1) * PIECE])
+        def times_gate(k):
+            s0, s1 = SCALAR_CUTS[k], SCALAR_CUTS[k + 1]
+            nc.vector.tensor_tensor(gated[:, s0:s1], y[1][:, s0:s1], gate_all[:, s0:s1], MULT)
 
-        for u in range(2):
+        def scatter_scalar(k):
+            s0, s1 = SCALAR_CUTS[k], SCALAR_CUTS[k + 1]
+            nc.scalar.activation(window1[:].indirect(slots(dst_t, s0, s1)), gated[:, s0:s1], COPY)
+
+        def scatter_vector(k):
+            s0, s1 = VECTOR_CUTS[k], VECTOR_CUTS[k + 1]
+            nc.vector.tensor_tensor(window0[:].indirect(slots(dst_t, s0, s1)), y[0][:, s0:s1], gate_all[:, s0:s1], MULT)
+
+        for u in range(3):
             round_pair(u)
-            step = (WIDE, PIECE)[u]
-            for s0 in range(0, SLOTS, step):
-                gather_words(pairs0[:, u, s0 : s0 + step], u, s0, s0 + step)
-        nc.gpsimd.tensor_copy(win_row[0][:], raw_c[:])
+            for s in range(2):
+                gather(u, s, 0, WIDE)
+        merge(nc.scalar.copy, U32, 0, 0, 0, PIECE)
+        round_pair(3)
+        merge(nc.scalar.copy, U32, 0, 0, PIECE, WIDE)
+        merge(nc.scalar.copy, U32, 0, 1, 0, PIECE)
+        gather(3, 0, 0, PIECE)
+        gather(3, 0, PIECE, WIDE)
+        quantise(0, 0, 0, WIDE)
         for i in range(2):
-            merge0(nc.scalar.copy, U32, i)
-        merge0(nc.vector.tensor_copy, I32, 2)
-        quantise(codes0_early[:], planes0_early[:], quads0_early[:].rearrange("p i s -> p (i s)"))
-        round_pair(2)
-        for i in range(PIECES):
-            gather_third(i)
-        nc.gpsimd.tensor_copy(win_row[1][:, 0 : T - TAIL], raw_d)
-        nc.gpsimd.tensor_copy(win_row[1][:, T - TAIL :], raw_tail)
-        merge0(nc.gpsimd.tensor_copy, I32, 3)
-        for e in range(2):
-            for i in range(2):
-                gather_row(e, i)
-        for e in range(2):
-            merge(nc.vector.tensor_copy, I32, quads1[0][:, e * PIECE : (e + 1) * PIECE], pairs1[0][:, :, e * C : (e + 1) * C])
-        for e in range(2):
-            cols = slice(e * C, (e + 1) * C)
-            quantise(codes1[0][:, cols], planes1[0][:, cols], quads1[0][:, e * PIECE : (e + 1) * PIECE])
-        codes0_late = keep.tile([P, WIDE], U32, name="quads1_0", align_bytes=64)
-        codes0 = codes0 + [codes0_late[:, 0:PIECE], codes0_late[:, PIECE:]]
-        quantise(codes0_late[:], planes0_late[:], quads0_late[:, 0 : 2 * WIDE])
-        merge1(1)
-        quantise(codes1[1][:], planes1[1][:], quads1[1])
+            merge(nc.scalar.copy, U32, 1, 0, i * PIECE, (i + 1) * PIECE)
+            quantise(1, 0, i * PIECE, (i + 1) * PIECE)
+        merge(nc.scalar.copy, U32, 0, 1, PIECE, WIDE)
+        gather(3, 1, 0, WIDE)
 
-        for i in range(PIECES):
-            acc = {}
-            g = max(g for g in range(len(WEIGHTS)) if WEIGHTS[g][0] <= i)
+        def products(h, i):
             for a in range(PASSES):
-                for h in range(HALVES):
-                    for e in range(2):
-                        if a == 0:
-                            acc[h, e] = psum.tile([P, C], F32, name=f"acc{h}_{e}")
-                        ws = ws_first[:, e * PASSES + a, :] if i == 0 else ws_rest[:, (2 * i + e - 2) * PASSES + a, :]
-                        c0 = e * C
-                        x = (2 * (i - WEIGHTS[g][0]) + e) * PASSES + a
-                        nc.tensor.matmul_mx(
-                            out=acc[h, e][:],
-                            lhsT=ww[g][:, x, h * 2 * P : (h + 1) * 2 * P].bitcast(FP4X4),
-                            lhsT_scale=ws[:, h * P : (h + 1) * P],
-                            rhs=(codes0[i], codes1[i])[a][:, c0 : c0 + C].bitcast(FP8X4),
-                            rhs_scale=(planes0[i], planes1[i])[a][:, c0 : c0 + C],
-                            start=(a == 0),
-                            stop=(a == PASSES - 1),
-                        )
-            for h in range(HALVES):
-                if h == 1 and 0 < i < PIECES - 1:
-                    merge1(i + 1)
-                    quantise(codes1[i + 1][:], planes1[i + 1][:], quads1[i + 1])
-                    y = unit(PLACES[i + 1][0])
-                else:
-                    y = keep.tile([P, PIECE], F32, name=f"y{h}_{i}")[:]
-                for e in range(2):
-                    nc.scalar.activation(
-                        y[:, e * C : (e + 1) * C], acc[h, e][:], RELU, bias=bias_of(h, i)[:, e : e + 1]
-                    )
-                nc.vector.tensor_tensor(
-                    out_t[h][:].indirect(slots(dst_t, i * PIECE, (i + 1) * PIECE)),
-                    y,
-                    gate_t[:, i * PIECE : (i + 1) * PIECE],
-                    MULT,
-                )
-            if i + 2 < PIECES:
-                for e in range(2):
-                    gather_row(e, i + 2)
-        for h in range(HALVES):
-            nc.sync.dma_start(out[h * P : (h + 1) * P, :], out_t[h][:])
+                for e in (2 * i, 2 * i + 1):
+                    multiply(a, h, e)
+
+        for h in (1, 0):
+            for i in range(2):
+                products(h, i)
+                for e in (2 * i, 2 * i + 1):
+                    activate(h, e)
+        times_gate(0)
+        scatter_scalar(0)
+        quantise(0, 1, 0, WIDE)
+        for i in range(2):
+            merge(nc.vector.tensor_copy, I32, 1, 1, i * PIECE, (i + 1) * PIECE)
+        for i in range(2):
+            quantise(1, 1, i * PIECE, (i + 1) * PIECE)
+        for h in (1, 0):
+            for i in range(2, 4):
+                products(h, i)
+        scatter_vector(0)
+        for h in (1, 0):
+            for e in range(STAGE, E):
+                activate(h, e)
+        for k in (1, 2):
+            times_gate(k)
+        for k in (1, 2):
+            scatter_scalar(k)
+            scatter_vector(k)
+        for h in (1, 0):
+            nc.sync.dma_start(out[h * P : (h + 1) * P, :], windows[h][:, 0:T])

@@ -10,7 +10,9 @@ PACK = 4
 PASSES = K // (P * PACK)
 HALVES = N // P
 PIECE = 2 * C
+PIECES = SLOTS // PIECE
 WIDE = 2 * PIECE
+REST = SLOTS - PIECE
 STAGE = E // 2
 
 F32 = mybir.dt.float32
@@ -24,10 +26,12 @@ FP4X4 = mybir.dt.float4_e2m1fn_x4
 COPY = mybir.ActivationFunctionType.Copy
 RELU = mybir.ActivationFunctionType.Relu
 MULT = mybir.AluOpType.mult
+ADD = mybir.AluOpType.add
+MAX = mybir.AluOpType.max
 
-LOADS = (((896, 576), (384, 208)), ((640, 0), (640, 320)), ((640, 0), (640, 320)), ((640, 0), (640, 320)))
-SCALAR_CUTS = (0, 384, 768, 1024)
-VECTOR_CUTS = (0, 288, 672, 1024)
+STREAMED = ((0, 0, 640), (0, 384, 0), (0, 128, 128))
+LAST = ((0, 0, 640), (0, 384, 0), (0, 256, 0))
+LOADS = (((576, 320, 0), (208, 176, 0)), STREAMED, STREAMED, LAST)
 WEIGHTS = ((0, 2), (2, 4), (4, 8))
 
 
@@ -42,54 +46,58 @@ def tile_moe_two_lin_relu_kernel(tc, xT, w_words, w_scales, b, gate, offs, dst, 
         ww = [keep.tile([P, (e1 - e0) * PASSES, 2 * N], U8, name=f"ww{e0}", align_bytes=256) for e0, e1 in WEIGHTS]
         ws = [keep.tile([P, STAGE * PASSES, N], U8, name=f"ws{s}", align_bytes=64) for s in range(2)]
         gate_all = keep.tile([P, SLOTS], F32, name="gate_all", align_bytes=256)
-        bias_t = keep.tile([P, HALVES, E], F32, name="bias_t")
-        window0 = keep.tile([P, T + 2 * WIDE], F32, name="window0", align_bytes=256)
-        window1 = keep.tile([P, T], F32, name="window1", align_bytes=256)
+        window0 = keep.tile([P, T], F32, name="window0", align_bytes=256)
+        window1 = keep.tile([P, T + HALVES * E], F32, name="window1", align_bytes=256)
         windows = (window0, window1)
-        late = keep.tile([P, 2 * SLOTS - SCALAR_CUTS[1]], F32, name="late", align_bytes=64)
-        y = [keep.tile([P, SLOTS], F32, name="y0", align_bytes=64)[:], late[:, SLOTS - SCALAR_CUTS[1] :]]
-        gated = keep.tile([P, SLOTS], F32, name="gated", align_bytes=64)
+        y = [keep.tile([P, SLOTS], F32, name=f"y{h}", align_bytes=64) for h in range(HALVES)]
+        gated = {
+            (h, i): keep.tile([P, PIECE], F32, name=f"gated{h}_{i}", align_bytes=64) for h in range(HALVES) for i in range(PIECES) if h == 1 or i < 2
+        }
 
-        last_loads = keep.tile([P, 2 * T + 2 * WIDE], F32, name="last_loads", align_bytes=256)
         raw = {
-            (u, c): keep.tile([P, 2 * LOADS[u][c][0]], F32, name=f"raw{u}_{c}", align_bytes=256)[:]
+            (u, c): keep.tile([P, 2 * sum(LOADS[u][c])], F32, name=f"raw{u}_{c}", align_bytes=256)[:]
             for u in range(4)
-            for c in range(2)
-            if u < 2 or c == 0
+            for c in range(len(LOADS[u]))
+            if u < 2 or c < 2
         }
-        raw[2, 1] = last_loads[:, 0:T]
-        raw[3, 1] = last_loads[:, T : 2 * T]
+        merged = keep.tile([P, 3 * WIDE], F32, name="merged", align_bytes=256)
+        raw[2, 2] = merged[:, PIECE : PIECE + WIDE]
+        raw[3, 2] = merged[:, 2 * WIDE :]
         win = [keep.tile([P, T, 2], BF16, name=f"win{u}") for u in range(4)]
-        pairs = {(0, s): keep.tile([P, 2 * WIDE], U32, name=f"pairs0_{s}", align_bytes=64)[:] for s in range(2)}
-        pairs[1, 0] = last_loads[:, 2 * T :].bitcast(U32)
-        pairs[1, 1] = window0[:, T:].bitcast(U32)
-        early = last_loads[:, T - WIDE : T + WIDE].bitcast(U32)
-        across = last_loads[:, 2 * T - WIDE : 2 * T + WIDE].bitcast(U32)
+        pairs0 = [keep.tile([P, 2 * WIDE], U32, name=f"pairs0_{s}", align_bytes=64) for s in range(2)]
+        pairs1_first = keep.tile([P, WIDE], U32, name="pairs1_first", align_bytes=64)[:]
+        rest = keep.tile([P, PIECE + 2 * REST], U32, name="rest", align_bytes=64)
+        pairs1_rest = rest[:, PIECE:]
+        parked = keep.tile([P, 2 * E + WIDE], F32, name="parked", align_bytes=64)
+        second = parked[:, 2 * E :]
         quads = {
-            (0, 0): early,
-            (0, 1): early[:, WIDE:],
-            (0, 2): across,
-            (0, 3): across[:, WIDE:],
-            (1, 0): pairs[1, 1][:, WIDE:],
-            (1, 1): keep.tile([P, WIDE], U32, name="quads1_1", align_bytes=64)[:],
-            (1, 2): late[:, 0:WIDE].bitcast(U32),
-            (1, 3): late[:, WIDE:SLOTS].bitcast(U32),
+            (0, 0): keep.tile([P, WIDE], U32, name="quads0_0", align_bytes=64)[:],
+            (0, 1): merged[:, 0:WIDE].bitcast(U32),
+            (0, 2): merged[:, WIDE:].bitcast(U32),
+            (0, 3): merged[:, 2 * WIDE :].bitcast(U32),
+            (1, 0): pairs1_rest[:, REST : REST + WIDE],
+            (1, 1): second.bitcast(U32),
+            (1, 2): rest[:, 0:WIDE],
+            (1, 3): second.bitcast(U32),
         }
-        codes = {(a, s): keep.tile([P, WIDE], U32, name=f"codes{a}_{s}", align_bytes=64) for a in range(PASSES) for s in range(2)}
-        planes = {(a, s): keep.tile([P, WIDE], U8, name=f"planes{a}_{s}", align_bytes=64) for a in range(PASSES) for s in range(2)}
+        codes = {}
+        planes = {}
 
         for s in range(2):
             nc.vector.memset(ws[s][:].rearrange("p x n -> p (x n)").bitcast(I32), 0)
         for h in range(HALVES):
             nc.gpsimd.memset(windows[h][:, 0:T], 0.0)
 
+        def first_token(u, c):
+            return sum(sum(shares) for shares in LOADS[u][0:c])
+
         x_rows = xT.rearrange("(u p j) t -> u p j t", p=P, j=PACK)
         for u in range(4):
             a, j = u // 2, 2 * (u % 2)
-            for c in range(2):
-                t0 = c * LOADS[u][0][0]
+            for c in range(len(LOADS[u])):
+                t0 = first_token(u, c)
                 nc.sync.dma_start(
-                    raw[u, c].rearrange("p (e t) -> p e t", e=2), x_rows[a, :, j : j + 2, t0 : t0 + LOADS[u][c][0]]
+                    raw[u, c].rearrange("p (e t) -> p e t", e=2), x_rows[a, :, j : j + 2, t0 : t0 + sum(LOADS[u][c])]
                 )
             if u == 0:
                 nc.sync.dma_start(offs_t[:], offs)
@@ -110,10 +118,11 @@ def tile_moe_two_lin_relu_kernel(tc, xT, w_words, w_scales, b, gate, offs, dst, 
 
         load_words(0)
         load_scales(0)
-        nc.sync.dma_start(bias_t[:], b.rearrange("(h p) e -> p h e", p=P))
+        nc.sync.dma_start(parked[:, E : 3 * E].rearrange("p (h e) -> p h e", h=HALVES), b.rearrange("(h p) e -> p h e", p=P))
         load_words(1)
         nc.sync.dma_start(gate_all[:, 0:WIDE], gate[0:P, 0:WIDE])
         nc.sync.dma_start(dst_t[:], dst)
+        nc.sync.dma_start(window1[:, T:].rearrange("p (h e) -> p h e", h=HALVES), b.rearrange("(h p) e -> p h e", p=P))
         load_words(2)
         load_scales(1)
         nc.sync.dma_start(gate_all[:, WIDE:], gate[0:P, WIDE:])
@@ -121,40 +130,64 @@ def tile_moe_two_lin_relu_kernel(tc, xT, w_words, w_scales, b, gate, offs, dst, 
         def scalar_cast(o, i):
             nc.scalar.activation(o, i, COPY)
 
+        def gpsimd_cast(o, i):
+            nc.gpsimd.tensor_copy(o, i)
+
         def slots(listed, s0, s1):
             return listed[:, s0 // 16 : s1 // 16]
 
         def interleave(copy, u, c, t0, t1):
-            first = c * LOADS[u][0][0]
+            first = first_token(u, c)
             copy(
                 win[u][:, first + t0 : first + t1, :],
                 raw[u, c].rearrange("p (e t) -> p t e", e=2)[:, t0:t1, :],
             )
 
         def round_pair(u):
-            for c in range(2):
-                n, v = LOADS[u][c]
-                if v > 0:
-                    interleave(nc.vector.tensor_copy, u, c, 0, v)
-                interleave(scalar_cast, u, c, v, n)
+            for c in range(len(LOADS[u])):
+                t0 = 0
+                for copy, n in zip((nc.vector.tensor_copy, scalar_cast, gpsimd_cast), LOADS[u][c]):
+                    if n > 0:
+                        interleave(copy, u, c, t0, t0 + n)
+                    t0 = t0 + n
 
-        def gather(u, s, s0, s1):
+        def gather(into, u, s0, n):
             window = win[u][:].rearrange("p t e -> p (t e)").bitcast(U32)
-            first = (u % 2) * WIDE
-            nc.vector.tensor_copy(
-                pairs[u // 2, s][:, first + s0 : first + s1], window.indirect(slots(offs_t, s * WIDE + s0, s * WIDE + s1))
-            )
+            nc.vector.tensor_copy(into, window.indirect(slots(offs_t, s0, s0 + n)))
 
-        def merge(copy, word, a, s, s0, s1):
+        def gather0(u, s0, n):
+            first = u * WIDE + s0 % WIDE
+            gather(pairs0[s0 // WIDE][:, first : first + n], u, s0, n)
+
+        def gather1(u, s0, n):
+            if s0 < PIECE:
+                first = u * PIECE + s0
+                gather(pairs1_first[:, first : first + n], 2 + u, s0, n)
+            else:
+                first = u * REST + s0 - PIECE
+                gather(pairs1_rest[:, first : first + n], 2 + u, s0, n)
+
+        def merge(copy, word, a, s0, n):
+            if a == 0:
+                both, first = pairs0[s0 // WIDE][:], s0 % WIDE
+            elif s0 < PIECE:
+                both, first = pairs1_first, s0
+            else:
+                both, first = pairs1_rest, s0 - PIECE
+            into = quads[a, s0 // PIECE][:, 2 * (s0 % PIECE) : 2 * (s0 % PIECE + n)]
             copy(
-                quads[a, 2 * s + s0 // PIECE][:, 0 : 2 * (s1 - s0)].bitcast(word).rearrange("p (s u) -> p s u", u=2),
-                pairs[a, s].bitcast(word).rearrange("p (u s) -> p s u", u=2)[:, s0:s1, :],
+                into.bitcast(word).rearrange("p (s u) -> p s u", u=2),
+                both.bitcast(word).rearrange("p (u s) -> p s u", u=2)[:, first : first + n, :],
             )
 
-        def quantise(a, s, s0, s1):
-            nc.vector.quantize_mx(
-                out=codes[a, s][:, s0:s1].bitcast(FP8X4), scales=planes[a, s][:, s0:s1], in_=quads[a, 2 * s + s0 // PIECE][:, 0 : 2 * (s1 - s0)].bitcast(BF16)
-            )
+        def quantise(a, s0, n, tag, align=64):
+            words = keep.tile([P, n], U32, name=tag, align_bytes=align)
+            scales = keep.tile([P, n], U8, name=f"planes{a}_{s0}", align_bytes=64)
+            for c0 in range(0, n, C):
+                codes[a, (s0 + c0) // C] = words[:, c0 : c0 + C]
+                planes[a, (s0 + c0) // C] = scales[:, c0 : c0 + C]
+            values = quads[a, s0 // PIECE][:, 2 * (s0 % PIECE) : 2 * (s0 % PIECE + n)]
+            nc.vector.quantize_mx(out=words[:].bitcast(FP8X4), scales=scales[:], in_=values.bitcast(BF16))
 
         acc = {}
 
@@ -169,72 +202,88 @@ def tile_moe_two_lin_relu_kernel(tc, xT, w_words, w_scales, b, gate, offs, dst, 
                 out=acc[h, e],
                 lhsT=ww[g][:, (e - WEIGHTS[g][0]) * PASSES + a, h * 2 * P : (h + 1) * 2 * P].bitcast(FP4X4),
                 lhsT_scale=ws[s][:, i * PASSES + a, h * P : (h + 1) * P],
-                rhs=codes[a, s][:, i * C : (i + 1) * C].bitcast(FP8X4),
-                rhs_scale=planes[a, s][:, i * C : (i + 1) * C],
+                rhs=codes[a, e].bitcast(FP8X4),
+                rhs_scale=planes[a, e],
                 start=(a == 0 and e % 2 == 0),
                 stop=(a == PASSES - 1 and e % 2 == 1),
             )
 
-        def activate(h, e):
-            nc.scalar.activation(y[h][:, e * C : (e + 1) * C], acc[h, e], RELU, bias=bias_t[:, h, e : e + 1])
+        def products(i):
+            for h in (1, 0):
+                for a in range(PASSES):
+                    for e in (2 * i, 2 * i + 1):
+                        multiply(a, h, e)
 
-        def times_gate(k):
-            s0, s1 = SCALAR_CUTS[k], SCALAR_CUTS[k + 1]
-            nc.vector.tensor_tensor(gated[:, s0:s1], y[1][:, s0:s1], gate_all[:, s0:s1], MULT)
+        def activate(h, i):
+            for e in (2 * i, 2 * i + 1):
+                into = y[h][:, e * C : (e + 1) * C]
+                if h == 0 and i > 1:
+                    nc.vector.tensor_scalar(into, acc[h, e], parked[:, E + e : E + e + 1], 0.0, ADD, MAX)
+                elif i > 0:
+                    nc.scalar.activation(into, acc[h, e], RELU, bias=window1[:, T + h * E + e : T + h * E + e + 1])
+                else:
+                    nc.scalar.activation(into, acc[h, e], RELU, bias=parked[:, (h + 1) * E + e : (h + 1) * E + e + 1])
+            cols = slice(i * PIECE, (i + 1) * PIECE)
+            if h == 1 or i < 2:
+                nc.gpsimd.tensor_tensor(gated[h, i][:], y[h][:, cols], gate_all[:, cols], MULT)
 
-        def scatter_scalar(k):
-            s0, s1 = SCALAR_CUTS[k], SCALAR_CUTS[k + 1]
-            nc.scalar.activation(window1[:].indirect(slots(dst_t, s0, s1)), gated[:, s0:s1], COPY)
+        def scatter(h, i):
+            s0, s1 = i * PIECE, (i + 1) * PIECE
+            places = windows[h][:].indirect(slots(dst_t, s0, s1))
+            if h == 1:
+                scalar_cast(places, gated[h, i][:])
+            elif i < 2:
+                nc.vector.tensor_copy(places, gated[h, i][:])
+            else:
+                nc.vector.tensor_tensor(places, y[h][:, s0:s1], gate_all[:, s0:s1], MULT)
 
-        def scatter_vector(k):
-            s0, s1 = VECTOR_CUTS[k], VECTOR_CUTS[k + 1]
-            nc.vector.tensor_tensor(window0[:].indirect(slots(dst_t, s0, s1)), y[0][:, s0:s1], gate_all[:, s0:s1], MULT)
-
-        for u in range(3):
-            round_pair(u)
-            for s in range(2):
-                gather(u, s, 0, WIDE)
-        merge(nc.scalar.copy, U32, 0, 0, 0, PIECE)
+        round_pair(0)
+        for s0 in (0, WIDE):
+            gather0(0, s0, WIDE)
+        round_pair(1)
+        gather0(1, 0, PIECE)
+        gather0(1, PIECE, PIECE)
+        gather0(1, WIDE, WIDE)
+        merge(nc.scalar.copy, U32, 0, 0, PIECE)
+        round_pair(2)
+        gather1(0, 0, PIECE)
+        gather1(0, PIECE, REST)
+        for i in (1, 2):
+            merge(nc.scalar.copy, U32, 0, i * PIECE, PIECE)
         round_pair(3)
-        merge(nc.scalar.copy, U32, 0, 0, PIECE, WIDE)
-        merge(nc.scalar.copy, U32, 0, 1, 0, PIECE)
-        gather(3, 0, 0, PIECE)
-        gather(3, 0, PIECE, WIDE)
-        quantise(0, 0, 0, WIDE)
-        for i in range(2):
-            merge(nc.scalar.copy, U32, 1, 0, i * PIECE, (i + 1) * PIECE)
-            quantise(1, 0, i * PIECE, (i + 1) * PIECE)
-        merge(nc.scalar.copy, U32, 0, 1, PIECE, WIDE)
-        gather(3, 1, 0, WIDE)
-
-        def products(h, i):
-            for a in range(PASSES):
-                for e in (2 * i, 2 * i + 1):
-                    multiply(a, h, e)
-
-        for h in (1, 0):
-            for i in range(2):
-                products(h, i)
-                for e in (2 * i, 2 * i + 1):
-                    activate(h, e)
-        times_gate(0)
-        scatter_scalar(0)
-        quantise(0, 1, 0, WIDE)
-        for i in range(2):
-            merge(nc.vector.tensor_copy, I32, 1, 1, i * PIECE, (i + 1) * PIECE)
-        for i in range(2):
-            quantise(1, 1, i * PIECE, (i + 1) * PIECE)
-        for h in (1, 0):
-            for i in range(2, 4):
-                products(h, i)
-        scatter_vector(0)
-        for h in (1, 0):
-            for e in range(STAGE, E):
-                activate(h, e)
-        for k in (1, 2):
-            times_gate(k)
-        for k in (1, 2):
-            scatter_scalar(k)
-            scatter_vector(k)
-        for h in (1, 0):
-            nc.sync.dma_start(out[h * P : (h + 1) * P, :], windows[h][:, 0:T])
+        quantise(0, 0, PIECE, "raw3_1", 256)
+        merge(nc.scalar.copy, U32, 0, 3 * PIECE, PIECE)
+        for e in range(2):
+            gather1(1, e * C, C)
+            merge(nc.scalar.copy, U32, 1, e * C, C)
+        quantise(0, PIECE, PIECE, "pairs0_1")
+        for e in range(2):
+            quantise(1, e * C, C, f"codes1_{e}")
+        gather1(1, PIECE, PIECE)
+        gather1(1, WIDE, WIDE)
+        products(0)
+        activate(1, 0)
+        merge(nc.scalar.copy, U32, 1, PIECE, PIECE)
+        activate(0, 0)
+        scatter(1, 0)
+        quantise(1, PIECE, PIECE, "codes1_2")
+        products(1)
+        quantise(0, WIDE, WIDE, "pairs1_first")
+        for i in range(2, PIECES):
+            merge(nc.vector.tensor_copy, I32, 1, i * PIECE, PIECE)
+        for i in range(2, PIECES):
+            quantise(1, i * PIECE, PIECE, f"codes1_{2 * i}")
+            products(i)
+        activate(1, 1)
+        activate(0, 1)
+        activate(1, 2)
+        scatter(1, 1)
+        activate(1, 3)
+        for i in range(2, PIECES):
+            scatter(1, i)
+            scatter(0, i - 2)
+            activate(0, i)
+        for i in range(2, PIECES):
+            scatter(0, i)
+        nc.scalar.dma_start(out[P:, :], window1[:, 0:T])
+        nc.sync.dma_start(out[0:P, :], window0[:])

@@ -29,9 +29,9 @@ MULT = mybir.AluOpType.mult
 ADD = mybir.AluOpType.add
 MAX = mybir.AluOpType.max
 
-STREAMED = ((0, 0, 640), (0, 384, 0), (0, 128, 128))
-LAST = ((0, 0, 640), (0, 384, 0), (0, 256, 0))
-LOADS = (((576, 320, 0), (208, 176, 0)), STREAMED, STREAMED, LAST)
+SECOND = ((0, 192, 448), (0, 384, 0), (0, 256, 0))
+LATER = ((0, 0, 640), (0, 384, 0), (0, 256, 0))
+LOADS = (((576, 320, 0), (208, 176, 0)), SECOND, LATER, LATER)
 WEIGHTS = ((0, 2), (2, 4), (4, 8))
 
 
@@ -46,7 +46,7 @@ def tile_moe_two_lin_relu_kernel(tc, xT, w_words, w_scales, b, gate, offs, dst, 
         ww = [keep.tile([P, (e1 - e0) * PASSES, 2 * N], U8, name=f"ww{e0}", align_bytes=256) for e0, e1 in WEIGHTS]
         ws = [keep.tile([P, STAGE * PASSES, N], U8, name=f"ws{s}", align_bytes=64) for s in range(2)]
         gate_all = keep.tile([P, SLOTS], F32, name="gate_all", align_bytes=256)
-        window0 = keep.tile([P, T], F32, name="window0", align_bytes=256)
+        window0 = keep.tile([P, T + E], F32, name="window0", align_bytes=256)
         window1 = keep.tile([P, T + HALVES * E], F32, name="window1", align_bytes=256)
         windows = (window0, window1)
         y = [keep.tile([P, SLOTS], F32, name=f"y{h}", align_bytes=64) for h in range(HALVES)]
@@ -58,23 +58,25 @@ def tile_moe_two_lin_relu_kernel(tc, xT, w_words, w_scales, b, gate, offs, dst, 
             (u, c): keep.tile([P, 2 * sum(LOADS[u][c])], F32, name=f"raw{u}_{c}", align_bytes=256)[:]
             for u in range(4)
             for c in range(len(LOADS[u]))
-            if u < 2 or c < 2
+            if (u, c) != (3, 2)
         }
-        merged = keep.tile([P, 3 * WIDE], F32, name="merged", align_bytes=256)
-        raw[2, 2] = merged[:, PIECE : PIECE + WIDE]
-        raw[3, 2] = merged[:, 2 * WIDE :]
-        win = [keep.tile([P, T, 2], BF16, name=f"win{u}") for u in range(4)]
+        merged = keep.tile([P, 2 * WIDE], F32, name="merged", align_bytes=256)
+        raw[3, 2] = merged[:, 0:WIDE]
+        win = [keep.tile([P, T, 2], BF16, name=f"win{u}", align_bytes=64) for u in range(4)]
         pairs0 = [keep.tile([P, 2 * WIDE], U32, name=f"pairs0_{s}", align_bytes=64) for s in range(2)]
-        pairs1_first = keep.tile([P, WIDE], U32, name="pairs1_first", align_bytes=64)[:]
+        pairs1_first = [
+            keep.tile([P, PIECE], U32, name="pairs1_first", align_bytes=64)[:],
+            merged[:, WIDE : WIDE + PIECE].bitcast(U32),
+        ]
         rest = keep.tile([P, PIECE + 2 * REST], U32, name="rest", align_bytes=64)
         pairs1_rest = rest[:, PIECE:]
         parked = keep.tile([P, 2 * E + WIDE], F32, name="parked", align_bytes=64)
         second = parked[:, 2 * E :]
         quads = {
             (0, 0): keep.tile([P, WIDE], U32, name="quads0_0", align_bytes=64)[:],
-            (0, 1): merged[:, 0:WIDE].bitcast(U32),
-            (0, 2): merged[:, WIDE:].bitcast(U32),
-            (0, 3): merged[:, 2 * WIDE :].bitcast(U32),
+            (0, 1): raw[2, 2].bitcast(U32),
+            (0, 2): merged[:].bitcast(U32),
+            (0, 3): merged[:, WIDE:].bitcast(U32),
             (1, 0): pairs1_rest[:, REST : REST + WIDE],
             (1, 1): second.bitcast(U32),
             (1, 2): rest[:, 0:WIDE],
@@ -126,12 +128,13 @@ def tile_moe_two_lin_relu_kernel(tc, xT, w_words, w_scales, b, gate, offs, dst, 
         load_words(2)
         load_scales(1)
         nc.sync.dma_start(gate_all[:, WIDE:], gate[0:P, WIDE:])
+        nc.sync.dma_start(window0[:, T:], b[0:P, :])
 
         def scalar_cast(o, i):
             nc.scalar.activation(o, i, COPY)
 
         def gpsimd_cast(o, i):
-            nc.gpsimd.tensor_copy(o, i)
+            nc.gpsimd.tensor_scalar(o, i, 1.0, 0.0, MULT, ADD)
 
         def slots(listed, s0, s1):
             return listed[:, s0 // 16 : s1 // 16]
@@ -161,8 +164,7 @@ def tile_moe_two_lin_relu_kernel(tc, xT, w_words, w_scales, b, gate, offs, dst, 
 
         def gather1(u, s0, n):
             if s0 < PIECE:
-                first = u * PIECE + s0
-                gather(pairs1_first[:, first : first + n], 2 + u, s0, n)
+                gather(pairs1_first[s0 // C][:, u * C : (u + 1) * C], 2 + u, s0, n)
             else:
                 first = u * REST + s0 - PIECE
                 gather(pairs1_rest[:, first : first + n], 2 + u, s0, n)
@@ -171,7 +173,7 @@ def tile_moe_two_lin_relu_kernel(tc, xT, w_words, w_scales, b, gate, offs, dst, 
             if a == 0:
                 both, first = pairs0[s0 // WIDE][:], s0 % WIDE
             elif s0 < PIECE:
-                both, first = pairs1_first, s0
+                both, first = pairs1_first[s0 // C], 0
             else:
                 both, first = pairs1_rest, s0 - PIECE
             into = quads[a, s0 // PIECE][:, 2 * (s0 % PIECE) : 2 * (s0 % PIECE + n)]
@@ -218,7 +220,7 @@ def tile_moe_two_lin_relu_kernel(tc, xT, w_words, w_scales, b, gate, offs, dst, 
             for e in (2 * i, 2 * i + 1):
                 into = y[h][:, e * C : (e + 1) * C]
                 if h == 0 and i > 1:
-                    nc.vector.tensor_scalar(into, acc[h, e], parked[:, E + e : E + e + 1], 0.0, ADD, MAX)
+                    nc.vector.tensor_scalar(into, acc[h, e], window0[:, T + e : T + e + 1], 0.0, ADD, MAX)
                 elif i > 0:
                     nc.scalar.activation(into, acc[h, e], RELU, bias=window1[:, T + h * E + e : T + h * E + e + 1])
                 else:
@@ -227,8 +229,8 @@ def tile_moe_two_lin_relu_kernel(tc, xT, w_words, w_scales, b, gate, offs, dst, 
             if h == 1 or i < 2:
                 nc.gpsimd.tensor_tensor(gated[h, i][:], y[h][:, cols], gate_all[:, cols], MULT)
 
-        def scatter(h, i):
-            s0, s1 = i * PIECE, (i + 1) * PIECE
+        def scatter(h, i, n=PIECE):
+            s0, s1 = i * PIECE, i * PIECE + n
             places = windows[h][:].indirect(slots(dst_t, s0, s1))
             if h == 1:
                 scalar_cast(places, gated[h, i][:])
@@ -241,22 +243,20 @@ def tile_moe_two_lin_relu_kernel(tc, xT, w_words, w_scales, b, gate, offs, dst, 
         for s0 in (0, WIDE):
             gather0(0, s0, WIDE)
         round_pair(1)
-        gather0(1, 0, PIECE)
-        gather0(1, PIECE, PIECE)
-        gather0(1, WIDE, WIDE)
-        merge(nc.scalar.copy, U32, 0, 0, PIECE)
+        for s0 in (0, WIDE):
+            gather0(1, s0, WIDE)
         round_pair(2)
-        gather1(0, 0, PIECE)
-        gather1(0, PIECE, REST)
-        for i in (1, 2):
+        for s0, n in ((0, C), (C, C), (PIECE, REST)):
+            gather1(0, s0, n)
+        for i in range(2):
             merge(nc.scalar.copy, U32, 0, i * PIECE, PIECE)
         round_pair(3)
-        quantise(0, 0, PIECE, "raw3_1", 256)
-        merge(nc.scalar.copy, U32, 0, 3 * PIECE, PIECE)
+        merge(nc.scalar.copy, U32, 0, WIDE, PIECE)
         for e in range(2):
             gather1(1, e * C, C)
             merge(nc.scalar.copy, U32, 1, e * C, C)
-        quantise(0, PIECE, PIECE, "pairs0_1")
+        merge(nc.scalar.copy, U32, 0, REST, PIECE)
+        quantise(0, 0, PIECE, "pairs1_first")
         for e in range(2):
             quantise(1, e * C, C, f"codes1_{e}")
         gather1(1, PIECE, PIECE)
@@ -266,9 +266,10 @@ def tile_moe_two_lin_relu_kernel(tc, xT, w_words, w_scales, b, gate, offs, dst, 
         merge(nc.scalar.copy, U32, 1, PIECE, PIECE)
         activate(0, 0)
         scatter(1, 0)
+        quantise(0, WIDE, WIDE, "codes0_4")
+        quantise(0, PIECE, PIECE, "win3")
         quantise(1, PIECE, PIECE, "codes1_2")
         products(1)
-        quantise(0, WIDE, WIDE, "pairs1_first")
         for i in range(2, PIECES):
             merge(nc.vector.tensor_copy, I32, 1, i * PIECE, PIECE)
         for i in range(2, PIECES):
@@ -279,11 +280,11 @@ def tile_moe_two_lin_relu_kernel(tc, xT, w_words, w_scales, b, gate, offs, dst, 
         activate(1, 2)
         scatter(1, 1)
         activate(1, 3)
+        scatter(0, 0)
         for i in range(2, PIECES):
             scatter(1, i)
-            scatter(0, i - 2)
             activate(0, i)
-        for i in range(2, PIECES):
-            scatter(0, i)
+        scatter(0, 1)
+        scatter(0, 2, WIDE)
         nc.scalar.dma_start(out[P:, :], window1[:, 0:T])
-        nc.sync.dma_start(out[0:P, :], window0[:])
+        nc.sync.dma_start(out[0:P, :], window0[:, 0:T])

@@ -26,12 +26,11 @@ FP4X4 = mybir.dt.float4_e2m1fn_x4
 COPY = mybir.ActivationFunctionType.Copy
 RELU = mybir.ActivationFunctionType.Relu
 MULT = mybir.AluOpType.mult
-ADD = mybir.AluOpType.add
-MAX = mybir.AluOpType.max
 
-SECOND = ((0, 192, 448), (0, 384, 0), (0, 256, 0))
-LATER = ((0, 0, 640), (0, 384, 0), (0, 256, 0))
-LOADS = (((576, 320, 0), (208, 176, 0)), SECOND, LATER, LATER)
+LATER = ((0, 448), (0, 448), (0, 384))
+LOADS = (((576, 320), (208, 176)), LATER, LATER, LATER)
+SCALAR_CUTS = (0, 256, 640, 1024)
+FIRST = 224
 WEIGHTS = ((0, 2), (2, 4), (4, 8))
 
 
@@ -46,13 +45,17 @@ def tile_moe_two_lin_relu_kernel(tc, xT, w_words, w_scales, b, gate, offs, dst, 
         ww = [keep.tile([P, (e1 - e0) * PASSES, 2 * N], U8, name=f"ww{e0}", align_bytes=256) for e0, e1 in WEIGHTS]
         ws = [keep.tile([P, STAGE * PASSES, N], U8, name=f"ws{s}", align_bytes=64) for s in range(2)]
         gate_all = keep.tile([P, SLOTS], F32, name="gate_all", align_bytes=256)
-        window0 = keep.tile([P, T + E], F32, name="window0", align_bytes=256)
+        window0 = keep.tile([P, 2 * (SLOTS - FIRST)], F32, name="window0", align_bytes=256)
         window1 = keep.tile([P, T + HALVES * E], F32, name="window1", align_bytes=256)
         windows = (window0, window1)
-        y = [keep.tile([P, SLOTS], F32, name=f"y{h}", align_bytes=64) for h in range(HALVES)]
-        gated = {
-            (h, i): keep.tile([P, PIECE], F32, name=f"gated{h}_{i}", align_bytes=64) for h in range(HALVES) for i in range(PIECES) if h == 1 or i < 2
-        }
+        y0 = keep.tile([P, SLOTS], F32, name="y0", align_bytes=64)
+        y1_first = keep.tile([P, PIECE], F32, name="y1_first", align_bytes=64)
+        y1_rest = keep.tile([P, REST], F32, name="y1_rest", align_bytes=64)
+        y = {(0, i): y0[:, i * PIECE :] for i in range(PIECES)}
+        y[1, 0] = y1_first[:]
+        for i in range(1, PIECES):
+            y[1, i] = y1_rest[:, (i - 1) * PIECE :]
+        gated = keep.tile([P, SLOTS], F32, name="gated", align_bytes=64)
 
         raw = {
             (u, c): keep.tile([P, 2 * sum(LOADS[u][c])], F32, name=f"raw{u}_{c}", align_bytes=256)[:]
@@ -60,28 +63,22 @@ def tile_moe_two_lin_relu_kernel(tc, xT, w_words, w_scales, b, gate, offs, dst, 
             for c in range(len(LOADS[u]))
             if (u, c) != (3, 2)
         }
-        merged = keep.tile([P, 2 * WIDE], F32, name="merged", align_bytes=256)
-        raw[3, 2] = merged[:, 0:WIDE]
+        merged = keep.tile([P, 4 * WIDE], F32, name="merged", align_bytes=256)
+        raw[3, 2] = merged[:, 320 : 320 + REST]
         win = [keep.tile([P, T, 2], BF16, name=f"win{u}", align_bytes=64) for u in range(4)]
         pairs0 = [keep.tile([P, 2 * WIDE], U32, name=f"pairs0_{s}", align_bytes=64) for s in range(2)]
         pairs1_first = [
             keep.tile([P, PIECE], U32, name="pairs1_first", align_bytes=64)[:],
-            merged[:, WIDE : WIDE + PIECE].bitcast(U32),
+            merged[:, 3 * WIDE : 3 * WIDE + PIECE].bitcast(U32),
         ]
-        rest = keep.tile([P, PIECE + 2 * REST], U32, name="rest", align_bytes=64)
-        pairs1_rest = rest[:, PIECE:]
-        parked = keep.tile([P, 2 * E + WIDE], F32, name="parked", align_bytes=64)
-        second = parked[:, 2 * E :]
-        quads = {
-            (0, 0): keep.tile([P, WIDE], U32, name="quads0_0", align_bytes=64)[:],
-            (0, 1): raw[2, 2].bitcast(U32),
-            (0, 2): merged[:].bitcast(U32),
-            (0, 3): merged[:, WIDE:].bitcast(U32),
-            (1, 0): pairs1_rest[:, REST : REST + WIDE],
-            (1, 1): second.bitcast(U32),
-            (1, 2): rest[:, 0:WIDE],
-            (1, 3): second.bitcast(U32),
-        }
+        rest = keep.tile([P, 2 * SLOTS], U32, name="rest", align_bytes=64)
+        pairs1_rest = rest[:, PIECE : PIECE + 2 * REST]
+        parked = rest[:, 3 * WIDE :].bitcast(F32)
+        quads = {(0, i): merged[:, i * WIDE :].bitcast(U32) for i in range(PIECES)}
+        quads[1, 0] = rest[:, SLOTS : SLOTS + WIDE]
+        quads[1, 1] = rest[:, 3 * WIDE :]
+        quads[1, 2] = rest[:, 0:WIDE]
+        quads[1, 3] = keep.tile([P, WIDE], U32, name="quads1_3", align_bytes=64)[:]
         codes = {}
         planes = {}
 
@@ -120,7 +117,7 @@ def tile_moe_two_lin_relu_kernel(tc, xT, w_words, w_scales, b, gate, offs, dst, 
 
         load_words(0)
         load_scales(0)
-        nc.sync.dma_start(parked[:, E : 3 * E].rearrange("p (h e) -> p h e", h=HALVES), b.rearrange("(h p) e -> p h e", p=P))
+        nc.sync.dma_start(parked[:, 0:2], b[P:, 0:2])
         load_words(1)
         nc.sync.dma_start(gate_all[:, 0:WIDE], gate[0:P, 0:WIDE])
         nc.sync.dma_start(dst_t[:], dst)
@@ -128,13 +125,9 @@ def tile_moe_two_lin_relu_kernel(tc, xT, w_words, w_scales, b, gate, offs, dst, 
         load_words(2)
         load_scales(1)
         nc.sync.dma_start(gate_all[:, WIDE:], gate[0:P, WIDE:])
-        nc.sync.dma_start(window0[:, T:], b[0:P, :])
 
         def scalar_cast(o, i):
             nc.scalar.activation(o, i, COPY)
-
-        def gpsimd_cast(o, i):
-            nc.gpsimd.tensor_scalar(o, i, 1.0, 0.0, MULT, ADD)
 
         def slots(listed, s0, s1):
             return listed[:, s0 // 16 : s1 // 16]
@@ -149,7 +142,7 @@ def tile_moe_two_lin_relu_kernel(tc, xT, w_words, w_scales, b, gate, offs, dst, 
         def round_pair(u):
             for c in range(len(LOADS[u])):
                 t0 = 0
-                for copy, n in zip((nc.vector.tensor_copy, scalar_cast, gpsimd_cast), LOADS[u][c]):
+                for copy, n in zip((nc.vector.tensor_copy, scalar_cast), LOADS[u][c]):
                     if n > 0:
                         interleave(copy, u, c, t0, t0 + n)
                     t0 = t0 + n
@@ -210,34 +203,28 @@ def tile_moe_two_lin_relu_kernel(tc, xT, w_words, w_scales, b, gate, offs, dst, 
                 stop=(a == PASSES - 1 and e % 2 == 1),
             )
 
-        def products(i):
+        def products(i, passes):
             for h in (1, 0):
-                for a in range(PASSES):
+                for a in passes:
                     for e in (2 * i, 2 * i + 1):
                         multiply(a, h, e)
 
         def activate(h, i):
             for e in (2 * i, 2 * i + 1):
-                into = y[h][:, e * C : (e + 1) * C]
-                if h == 0 and i > 1:
-                    nc.vector.tensor_scalar(into, acc[h, e], window0[:, T + e : T + e + 1], 0.0, ADD, MAX)
-                elif i > 0:
-                    nc.scalar.activation(into, acc[h, e], RELU, bias=window1[:, T + h * E + e : T + h * E + e + 1])
-                else:
-                    nc.scalar.activation(into, acc[h, e], RELU, bias=parked[:, (h + 1) * E + e : (h + 1) * E + e + 1])
-            cols = slice(i * PIECE, (i + 1) * PIECE)
-            if h == 1 or i < 2:
-                nc.gpsimd.tensor_tensor(gated[h, i][:], y[h][:, cols], gate_all[:, cols], MULT)
+                held = parked if (h, i) == (1, 0) else window1[:, T + h * E :]
+                nc.scalar.activation(y[h, i][:, (e % 2) * C : (e % 2 + 1) * C], acc[h, e], RELU, bias=held[:, e : e + 1])
 
-        def scatter(h, i, n=PIECE):
-            s0, s1 = i * PIECE, i * PIECE + n
-            places = windows[h][:].indirect(slots(dst_t, s0, s1))
-            if h == 1:
-                scalar_cast(places, gated[h, i][:])
-            elif i < 2:
-                nc.vector.tensor_copy(places, gated[h, i][:])
-            else:
-                nc.vector.tensor_tensor(places, y[h][:, s0:s1], gate_all[:, s0:s1], MULT)
+        def times_gate(k):
+            s0, s1 = SCALAR_CUTS[k], SCALAR_CUTS[k + 1]
+            values = y1_first[:] if k == 0 else y1_rest[:, s0 - PIECE : s1 - PIECE]
+            nc.vector.tensor_tensor(gated[:, s0:s1], values, gate_all[:, s0:s1], MULT)
+
+        def scatter_scalar(k):
+            s0, s1 = SCALAR_CUTS[k], SCALAR_CUTS[k + 1]
+            scalar_cast(window1[:].indirect(slots(dst_t, s0, s1)), gated[:, s0:s1])
+
+        def scatter_vector(s0, s1):
+            nc.vector.tensor_tensor(window0[:].indirect(slots(dst_t, s0, s1)), y0[:, s0:s1], gate_all[:, s0:s1], MULT)
 
         round_pair(0)
         for s0 in (0, WIDE):
@@ -248,43 +235,48 @@ def tile_moe_two_lin_relu_kernel(tc, xT, w_words, w_scales, b, gate, offs, dst, 
         round_pair(2)
         for s0, n in ((0, C), (C, C), (PIECE, REST)):
             gather1(0, s0, n)
-        for i in range(2):
-            merge(nc.scalar.copy, U32, 0, i * PIECE, PIECE)
         round_pair(3)
-        merge(nc.scalar.copy, U32, 0, WIDE, PIECE)
+        merge(nc.scalar.copy, U32, 0, 0, PIECE)
         for e in range(2):
             gather1(1, e * C, C)
             merge(nc.scalar.copy, U32, 1, e * C, C)
-        merge(nc.scalar.copy, U32, 0, REST, PIECE)
-        quantise(0, 0, PIECE, "pairs1_first")
+        for i in (1, 2):
+            merge(nc.scalar.copy, U32, 0, i * PIECE, PIECE)
+        quantise(0, 0, PIECE, "codes0_0")
         for e in range(2):
             quantise(1, e * C, C, f"codes1_{e}")
         gather1(1, PIECE, PIECE)
-        gather1(1, WIDE, WIDE)
-        products(0)
+        merge(nc.vector.tensor_copy, I32, 0, REST, PIECE)
+        gather1(1, WIDE, PIECE)
+        products(0, (0, 1))
         activate(1, 0)
+        times_gate(0)
         merge(nc.scalar.copy, U32, 1, PIECE, PIECE)
         activate(0, 0)
-        scatter(1, 0)
+        scatter_scalar(0)
         quantise(0, WIDE, WIDE, "codes0_4")
-        quantise(0, PIECE, PIECE, "win3")
+        for i in range(2, PIECES):
+            products(i, (0,))
         quantise(1, PIECE, PIECE, "codes1_2")
-        products(1)
+        quantise(0, PIECE, PIECE, "y1_first")
+        products(1, (0, 1))
+        gather1(1, REST, PIECE)
         for i in range(2, PIECES):
             merge(nc.vector.tensor_copy, I32, 1, i * PIECE, PIECE)
         for i in range(2, PIECES):
             quantise(1, i * PIECE, PIECE, f"codes1_{2 * i}")
-            products(i)
+            products(i, (1,))
         activate(1, 1)
-        activate(0, 1)
         activate(1, 2)
-        scatter(1, 1)
+        activate(0, 1)
         activate(1, 3)
-        scatter(0, 0)
         for i in range(2, PIECES):
-            scatter(1, i)
             activate(0, i)
-        scatter(0, 1)
-        scatter(0, 2, WIDE)
+        scatter_vector(0, FIRST)
+        for k in (1, 2):
+            times_gate(k)
+        for k in (1, 2):
+            scatter_scalar(k)
+        scatter_vector(FIRST, SLOTS)
         nc.scalar.dma_start(out[P:, :], window1[:, 0:T])
         nc.sync.dma_start(out[0:P, :], window0[:, 0:T])

from contextlib import ExitStack

import concourse.mybir as mybir

K, T, E, C, N = 1024, 1280, 8, 128, 256
SLOTS = E * C
FLOPS = 2 * K * SLOTS * N
P = 128
PACK = 4
PASSES = K // (P * PACK)
HALVES = N // P
PIECE = 2 * C
PIECES = SLOTS // PIECE
WIDE = 2 * PIECE
REST = SLOTS - PIECE
STAGE = E // 2

F32 = mybir.dt.float32
BF16 = mybir.dt.bfloat16
I32 = mybir.dt.int32
U32 = mybir.dt.uint32
U16 = mybir.dt.uint16
U8 = mybir.dt.uint8
FP8X4 = mybir.dt.float8_e4m3fn_x4
FP4X4 = mybir.dt.float4_e2m1fn_x4
COPY = mybir.ActivationFunctionType.Copy
RELU = mybir.ActivationFunctionType.Relu
MULT = mybir.AluOpType.mult

LATER = ((0, 448), (0, 448), (0, 384))
LOADS = (((576, 320), (208, 176)), LATER, LATER, LATER)
SCALAR_CUTS = (0, 256, 640, 1024)
FIRST = 224
WEIGHTS = ((0, 2), (2, 4), (4, 8))


def tile_moe_two_lin_relu_kernel(tc, xT, w_words, w_scales, b, gate, offs, dst, out):
    nc = tc.nc
    with ExitStack() as ctx:
        keep = ctx.enter_context(tc.tile_pool(name="keep", bufs=1))
        psum = ctx.enter_context(tc.psum_pool(name="psum", bufs=1))

        offs_t = keep.tile([P, SLOTS // 16], U16, name="offs_t")
        dst_t = keep.tile([P, SLOTS // 16], U16, name="dst_t")
        ww = [keep.tile([P, (e1 - e0) * PASSES, 2 * N], U8, name=f"ww{e0}", align_bytes=256) for e0, e1 in WEIGHTS]
        ws = [keep.tile([P, STAGE * PASSES, N], U8, name=f"ws{s}", align_bytes=64) for s in range(2)]
        gate_all = keep.tile([P, SLOTS], F32, name="gate_all", align_bytes=256)
        window0 = keep.tile([P, 2 * (SLOTS - FIRST)], F32, name="window0", align_bytes=256)
        window1 = keep.tile([P, T + HALVES * E], F32, name="window1", align_bytes=256)
        windows = (window0, window1)
        y0 = keep.tile([P, SLOTS], F32, name="y0", align_bytes=64)
        y1_first = keep.tile([P, PIECE], F32, name="y1_first", align_bytes=64)
        y1_rest = keep.tile([P, REST], F32, name="y1_rest", align_bytes=64)
        y = {(0, i): y0[:, i * PIECE :] for i in range(PIECES)}
        y[1, 0] = y1_first[:]
        for i in range(1, PIECES):
            y[1, i] = y1_rest[:, (i - 1) * PIECE :]
        gated = keep.tile([P, SLOTS], F32, name="gated", align_bytes=64)

        raw = {
            (u, c): keep.tile([P, 2 * sum(LOADS[u][c])], F32, name=f"raw{u}_{c}", align_bytes=256)[:]
            for u in range(4)
            for c in range(len(LOADS[u]))
            if (u, c) != (3, 2)
        }
        merged = keep.tile([P, 4 * WIDE], F32, name="merged", align_bytes=256)
        raw[3, 2] = merged[:, 320 : 320 + REST]
        win = [keep.tile([P, T, 2], BF16, name=f"win{u}", align_bytes=64) for u in range(4)]
        pairs0 = [keep.tile([P, 2 * WIDE], U32, name=f"pairs0_{s}", align_bytes=64) for s in range(2)]
        pairs1_first = [
            keep.tile([P, PIECE], U32, name="pairs1_first", align_bytes=64)[:],
            merged[:, 3 * WIDE : 3 * WIDE + PIECE].bitcast(U32),
        ]
        rest = keep.tile([P, 2 * SLOTS], U32, name="rest", align_bytes=64)
        pairs1_rest = rest[:, PIECE : PIECE + 2 * REST]
        parked = rest[:, 3 * WIDE :].bitcast(F32)
        quads = {(0, i): merged[:, i * WIDE :].bitcast(U32) for i in range(PIECES)}
        quads[1, 0] = rest[:, SLOTS : SLOTS + WIDE]
        quads[1, 1] = rest[:, 3 * WIDE :]
        quads[1, 2] = rest[:, 0:WIDE]
        quads[1, 3] = keep.tile([P, WIDE], U32, name="quads1_3", align_bytes=64)[:]
        codes = {}
        planes = {}

        for s in range(2):
            nc.vector.memset(ws[s][:].rearrange("p x n -> p (x n)").bitcast(I32), 0)
        for h in range(HALVES):
            nc.gpsimd.memset(windows[h][:, 0:T], 0.0)

        def first_token(u, c):
            return sum(sum(shares) for shares in LOADS[u][0:c])

        x_rows = xT.rearrange("(u p j) t -> u p j t", p=P, j=PACK)
        for u in range(4):
            a, j = u // 2, 2 * (u % 2)
            for c in range(len(LOADS[u])):
                t0 = first_token(u, c)
                nc.sync.dma_start(
                    raw[u, c].rearrange("p (e t) -> p e t", e=2), x_rows[a, :, j : j + 2, t0 : t0 + sum(LOADS[u][c])]
                )
            if u == 0:
                nc.sync.dma_start(offs_t[:], offs)

        s_rows = w_scales.rearrange("e a q n -> q (e a) n")
        w_rows = w_words.rearrange("e a p n -> p (e a) n")

        def load_scales(s):
            for q in range(4):
                nc.sync.dma_start(
                    ws[s][32 * q : 32 * q + 4, :, :].bitcast(I32),
                    s_rows[4 * q : 4 * q + 4, s * STAGE * PASSES : (s + 1) * STAGE * PASSES, :].bitcast(I32),
                )

        def load_words(g):
            e0, e1 = WEIGHTS[g]
            nc.sync.dma_start(ww[g][:].bitcast(I32), w_rows[:, PASSES * e0 : PASSES * e1, :].bitcast(I32))

        load_words(0)
        load_scales(0)
        nc.sync.dma_start(parked[:, 0:2], b[P:, 0:2])
        load_words(1)
        nc.sync.dma_start(gate_all[:, 0:WIDE], gate[0:P, 0:WIDE])
        nc.sync.dma_start(dst_t[:], dst)
        nc.sync.dma_start(window1[:, T:].rearrange("p (h e) -> p h e", h=HALVES), b.rearrange("(h p) e -> p h e", p=P))
        load_words(2)
        load_scales(1)
        nc.sync.dma_start(gate_all[:, WIDE:], gate[0:P, WIDE:])

        def scalar_cast(o, i):
            nc.scalar.activation(o, i, COPY)

        def slots(listed, s0, s1):
            return listed[:, s0 // 16 : s1 // 16]

        def interleave(copy, u, c, t0, t1):
            first = first_token(u, c)
            copy(
                win[u][:, first + t0 : first + t1, :],
                raw[u, c].rearrange("p (e t) -> p t e", e=2)[:, t0:t1, :],
            )

        def round_pair(u):
            for c in range(len(LOADS[u])):
                t0 = 0
                for copy, n in zip((nc.vector.tensor_copy, scalar_cast), LOADS[u][c]):
                    if n > 0:
                        interleave(copy, u, c, t0, t0 + n)
                    t0 = t0 + n

        def gather(into, u, s0, n):
            window = win[u][:].rearrange("p t e -> p (t e)").bitcast(U32)
            nc.vector.tensor_copy(into, window.indirect(slots(offs_t, s0, s0 + n)))

        def gather0(u, s0, n):
            first = u * WIDE + s0 % WIDE
            gather(pairs0[s0 // WIDE][:, first : first + n], u, s0, n)

        def gather1(u, s0, n):
            if s0 < PIECE:
                gather(pairs1_first[s0 // C][:, u * C : (u + 1) * C], 2 + u, s0, n)
            else:
                first = u * REST + s0 - PIECE
                gather(pairs1_rest[:, first : first + n], 2 + u, s0, n)

        def merge(copy, word, a, s0, n):
            if a == 0:
                both, first = pairs0[s0 // WIDE][:], s0 % WIDE
            elif s0 < PIECE:
                both, first = pairs1_first[s0 // C], 0
            else:
                both, first = pairs1_rest, s0 - PIECE
            into = quads[a, s0 // PIECE][:, 2 * (s0 % PIECE) : 2 * (s0 % PIECE + n)]
            copy(
                into.bitcast(word).rearrange("p (s u) -> p s u", u=2),
                both.bitcast(word).rearrange("p (u s) -> p s u", u=2)[:, first : first + n, :],
            )

        def quantise(a, s0, n, tag, align=64):
            words = keep.tile([P, n], U32, name=tag, align_bytes=align)
            scales = keep.tile([P, n], U8, name=f"planes{a}_{s0}", align_bytes=64)
            for c0 in range(0, n, C):
                codes[a, (s0 + c0) // C] = words[:, c0 : c0 + C]
                planes[a, (s0 + c0) // C] = scales[:, c0 : c0 + C]
            values = quads[a, s0 // PIECE][:, 2 * (s0 % PIECE) : 2 * (s0 % PIECE + n)]
            nc.vector.quantize_mx(out=words[:].bitcast(FP8X4), scales=scales[:], in_=values.bitcast(BF16))

        acc = {}

        def multiply(a, h, e):
            s, i = divmod(e, STAGE)
            g = max(g for g in range(len(WEIGHTS)) if WEIGHTS[g][0] <= e)
            if a == 0 and e % 2 == 0:
                bank = psum.tile([P, PIECE], F32, name=f"acc{h}_{e // 2}")
                acc[h, e] = bank[:, 0:C]
                acc[h, e + 1] = bank[:, C:]
            nc.tensor.matmul_mx(
                out=acc[h, e],
                lhsT=ww[g][:, (e - WEIGHTS[g][0]) * PASSES + a, h * 2 * P : (h + 1) * 2 * P].bitcast(FP4X4),
                lhsT_scale=ws[s][:, i * PASSES + a, h * P : (h + 1) * P],
                rhs=codes[a, e].bitcast(FP8X4),
                rhs_scale=planes[a, e],
                start=(a == 0 and e % 2 == 0),
                stop=(a == PASSES - 1 and e % 2 == 1),
            )

        def products(i, passes):
            for h in (1, 0):
                for a in passes:
                    for e in (2 * i, 2 * i + 1):
                        multiply(a, h, e)

        def activate(h, i):
            for e in (2 * i, 2 * i + 1):
                held = parked if (h, i) == (1, 0) else window1[:, T + h * E :]
                nc.scalar.activation(y[h, i][:, (e % 2) * C : (e % 2 + 1) * C], acc[h, e], RELU, bias=held[:, e : e + 1])

        def times_gate(k):
            s0, s1 = SCALAR_CUTS[k], SCALAR_CUTS[k + 1]
            values = y1_first[:] if k == 0 else y1_rest[:, s0 - PIECE : s1 - PIECE]
            nc.vector.tensor_tensor(gated[:, s0:s1], values, gate_all[:, s0:s1], MULT)

        def scatter_scalar(k):
            s0, s1 = SCALAR_CUTS[k], SCALAR_CUTS[k + 1]
            scalar_cast(window1[:].indirect(slots(dst_t, s0, s1)), gated[:, s0:s1])

        def scatter_vector(s0, s1):
            nc.vector.tensor_tensor(window0[:].indirect(slots(dst_t, s0, s1)), y0[:, s0:s1], gate_all[:, s0:s1], MULT)

        round_pair(0)
        for s0 in (0, WIDE):
            gather0(0, s0, WIDE)
        round_pair(1)
        for s0 in (0, WIDE):
            gather0(1, s0, WIDE)
        round_pair(2)
        for s0, n in ((0, C), (C, C), (PIECE, REST)):
            gather1(0, s0, n)
        round_pair(3)
        merge(nc.scalar.copy, U32, 0, 0, PIECE)
        for e in range(2):
            gather1(1, e * C, C)
            merge(nc.scalar.copy, U32, 1, e * C, C)
        for i in (1, 2):
            merge(nc.scalar.copy, U32, 0, i * PIECE, PIECE)
        quantise(0, 0, PIECE, "codes0_0")
        for e in range(2):
            quantise(1, e * C, C, f"codes1_{e}")
        gather1(1, PIECE, PIECE)
        merge(nc.vector.tensor_copy, I32, 0, REST, PIECE)
        gather1(1, WIDE, PIECE)
        products(0, (0, 1))
        activate(1, 0)
        times_gate(0)
        merge(nc.scalar.copy, U32, 1, PIECE, PIECE)
        activate(0, 0)
        scatter_scalar(0)
        quantise(0, WIDE, WIDE, "codes0_4")
        for i in range(2, PIECES):
            products(i, (0,))
        quantise(1, PIECE, PIECE, "codes1_2")
        quantise(0, PIECE, PIECE, "y1_first")
        products(1, (0, 1))
        gather1(1, REST, PIECE)
        for i in range(2, PIECES):
            merge(nc.vector.tensor_copy, I32, 1, i * PIECE, PIECE)
        for i in range(2, PIECES):
            quantise(1, i * PIECE, PIECE, f"codes1_{2 * i}")
            products(i, (1,))
        activate(1, 1)
        activate(1, 2)
        activate(0, 1)
        activate(1, 3)
        for i in range(2, PIECES):
            activate(0, i)
        scatter_vector(0, FIRST)
        for k in (1, 2):
            times_gate(k)
        for k in (1, 2):
            scatter_scalar(k)
        scatter_vector(FIRST, SLOTS)
        nc.scalar.dma_start(out[P:, :], window1[:, 0:T])
        nc.sync.dma_start(out[0:P, :], window0[:, 0:T])
